import numpy as np, ml_dtypes
CORES = [6,15,38,47]
N = 4
BF = ml_dtypes.bfloat16
def gentries(a):
    return np.ascontiguousarray(a.reshape(8, 16, -1).transpose(0, 2, 1)).reshape(8, -1)
def gtable(e):
    e = np.asarray(e); return np.ascontiguousarray(e.reshape(8, -1, 16).transpose(0, 2, 1)).reshape(128, -1).astype(np.int32)
W, B, L, S, RO, ST = 4096, 1024, 256, 16, 5, 1
def parts(rng):
    X = rng.integers(0, 201, (N, 8, 1, W)) + rng.integers(0, 56, (N, 8, 16, W))
    c = rng.integers(0, 101, (N, 8, 1, L)) + rng.integers(0, 56, (N, 8, 16, L))
    return X, rng.integers(0, W, (N, 8, 16, B)), rng.integers(0, W, (N, 8, 16, L)), c, rng.integers(0, B, (N, 8, L))
def pack(X, TT, T, c, b):
    return {"clk": X.reshape(N, 128, W).astype(np.float32).astype(BF), "ttab": TT.reshape(N, 128, B).astype(np.int32), "trav": T.reshape(N, 128, L).astype(np.int32),
            "last": c.reshape(N, 128, L).astype(np.float32).astype(BF), "slot": np.stack([gtable(a) for a in b])}
def setup_inputs(rng):
    return pack(*parts(rng))
def setup_inputs_spread(rng):
    pw = rng.choice(np.array([0.25, 0.5, 1.0, 2.0, 4.0]), (N, 8, 1, 1))
    sz = np.exp2(rng.integers(0, 8, (N, 8, 1, W)))
    X = np.clip(np.floor(256 * rng.random((N, 8, 1, W)) ** pw + sz * (rng.random((N, 8, 16, W)) - 0.5)), 0, 255).astype(np.int64)
    c = np.minimum(np.floor(256 * rng.random((N, 8, 1, L)) ** 2 * rng.random((N, 8, 16, L))), 255).astype(np.int64)
    pt = rng.choice(np.array([0.5, 1.0, 3.0]), (N, 8, 16, 1))
    T = np.minimum(np.floor(W * rng.random((N, 8, 16, L)) ** pt), W - 1).astype(np.int64)
    TT = np.minimum(np.floor(W * rng.random((N, 8, 16, B)) ** pt[::-1]), W - 1).astype(np.int64)
    b = np.minimum(np.floor(B * rng.random((N, 8, L)) ** 2), B - 1).astype(np.int64)
    return pack(X, TT, T, c, b)
def setup_inputs_ends(rng):
    X = 255 * rng.integers(0, 2, (N, 8, 16, W)); TT = (W - 1) * rng.integers(0, 2, (N, 8, 16, B)); T = (W - 1) * rng.integers(0, 2, (N, 8, 16, L))
    c = 255 * rng.integers(0, 2, (N, 8, 16, L)); b = (B - 1) * rng.integers(0, 2, (N, 8, L))
    for q in range(N):
        for g, size in ((3, 1), (7, 4)):
            P = np.sort(np.append(rng.permutation(15)[:size - 1], 15)); v = np.zeros(16, np.int64); v[P] = 255
            X[q, g] = (255 - v)[:, None]
            if size > 1:
                for t in (0, W - 1):
                    for s in (0, B - 1): X[q, g, int(np.argmin(v)), (((t * 511) >> 3) + 613 * int(P[0]) + 37 * s) & (W - 1)] = 254
            X[q, g, :, 0] = v; X[q, g, :, W - 1] = v
            c[q, g, P] = 255 * (np.arange(L) % 4 == 1)
            T[q, g, :, L - 1] = W - 1; b[q, g, L - 1] = B - 1
        X[q, 5] = 255; c[q, 5] = 0
        X[q, 6] = 255; c[q, 6] = 255
        if q % 2: c[q, 6, 15, L - 1] = 0
    return pack(X, TT, T, c, b)
def setup_inputs_corners(rng):
    X, TT, T, c, b = parts(rng); j = np.arange(W); i = np.arange(L)
    T[:, 0] = np.where(i % 2 == 0, 0, W - 1); b[:, 0] = np.where(i % 3 == 0, 0, B - 1)
    T[:, 1] = rng.integers(0, W, (N, 1, L))
    same = rng.integers(0, W, (N, 16, 1)); T[:, 2] = same; TT[:, 2] = same
    c[:, 3] = 255; b[:, 3] = (B - 99 + rng.integers(0, 100, (N, L))) & (B - 1)
    X[:, 4] = np.maximum(X[:, 4], 1); c[:, 4] = 0
    r = rng.integers(1, 255, (N, 16, 1)); X[:, 5] = r; c[:, 5] = r + rng.integers(-1, 2, (N, 16, L))
    o = np.argsort(rng.random((N, 16, W)), axis=1)
    X[:, 6] = np.where(j % 4 == 0, 100, np.where(j % 4 == 2, np.where(o < rng.integers(11, 13, (N, 1, W)), 120, 50), np.where(o < rng.integers(8, 11, (N, 1, W)), 101, 99)))
    T[:, 6] = 4 * rng.integers(0, W // 4, (N, 16, L)); TT[:, 6] = 2 * rng.integers(0, W // 2, (N, 16, B)) + 1; c[:, 6] = 0
    T[:, 7] = np.where(rng.random((N, 16, L)) < 0.5, (W - 1) * rng.integers(0, 2, (N, 16, L)), T[:, 7]); b[:, 7] = np.where(rng.random((N, L)) < 0.5, B - 1, b[:, 7])
    for a in (X, TT, T, c, b):
        for q in range(N): a[q] = np.roll(a[q], q, axis=0)
    return pack(X, TT, T, c, b)
def setup_inputs_crowd(rng):
    X, TT, T, c, b = parts(rng); one = rng.integers(0, B, (N, 8)); i = np.arange(L)
    for g in (0, 1, 2, 7): b[:, g] = one[:, g, None]
    b[:, 1, 0] = (one[:, 1] + 1) & (B - 1); b[:, 2, L - 1] = (one[:, 2] + 1) & (B - 1)
    b[:, 3] = one[:, 3, None] ^ rng.integers(0, 4, (N, L))
    b[:, 4] = B - 1; T[:, 4] = T[:, 4, :, :1].copy(); c[:, 4] = 255
    b[:, 5] = np.where(i % 2 == 0, one[:, 5, None], B - 1 - one[:, 5, None])
    b[:, 6] = 0; T[:, 6] = T[:, 6, :, :1].copy(); c[:, 6] = 255; c[:, 6, :, L - 1] = 0; X[:, 6] = np.maximum(X[:, 6], 1)
    for q in range(N):
        z = int(rng.integers(0, W)); X[q, 6, :, z] = 1; T[q, 6, :, L - 1] = z; TT[q, 6, :, 0] = z
    T[:, 7] = T[:, 7, :, :1].copy(); c[:, 7] = 0
    return pack(X, TT, T, c, b)
def high(rng, X, TT, T, c, g):
    o = np.argsort(rng.random((N, 16, W)), axis=1)
    X[:, g] = 255 - ((o < rng.integers(3, 7, (N, 1, W))) & (np.arange(W) % 2 == 1))
    T[:, g] = 2 * rng.integers(0, W // 2, (N, 16, L)); TT[:, g] = 2 * rng.integers(0, W // 2, (N, 16, B)); c[:, g] = rng.integers(253, 256, (N, 16, L))
def near(rng, X, TT, T, c, b, g):
    t = np.arange(W); v = np.zeros(16, np.int64); v[0] = 255; v[15] = 255
    for q in range(N):
        s = rng.permutation(B)[:L]; two = []
        for p, lo, hi in ((0, W - 8, W - 1), (15, 0, 8)):
            n = (((t * 511) >> 3)[None, :] + 613 * p + 37 * s[:, None]) & (W - 1)
            ok = (n >= lo) & (n <= hi) & (t > 8) & (t < W - 8)
            two.append(np.argmax(ok * rng.random((L, W)), axis=1))
        X[q, g] = (255 - v)[:, None]; X[q, g, 1, W - 8:] = 254
        for a in two: X[q, g][:, a] = v[:, None]
        T[q, g, :8] = two[0]; T[q, g, 8:] = two[1]; TT[q, g][:, s] = T[q, g]; b[q, g] = s
        c[q, g, 0] = rng.integers(0, 255, L); c[q, g, 15] = rng.integers(0, 255, L)
def setup_inputs_ties(rng):
    X, TT, T, c, b = parts(rng); o = rng.permutation(8)
    base = np.array([0, 0, 1, 64, 127, 127, 252, 252])[o].reshape(1, 8, 1, 1)
    X = base + rng.integers(0, 3, (N, 8, 1, W)) + (rng.random((N, 8, 16, W)) < 0.25)
    c = base + rng.integers(0, 2, (N, 8, 16, L))
    few = rng.integers(0, W, 8); T[:, ::2] = few[rng.integers(0, 8, (N, 4, 16, L))]
    high(rng, X, TT, T, c, int(np.argmax(o == 7))); near(rng, X, TT, T, c, b, int(np.argmax(o == 5)))
    return pack(X, TT, T, c, b)
def check_inputs(d):
    bad = []
    for k, lo, hi in (("clk", 0, 255), ("ttab", 0, W - 1), ("trav", 0, W - 1), ("last", 0, 255), ("slot", 0, B - 1)):
        a = np.asarray(d[k]).astype(np.float64)
        if not (np.min(a) >= lo and np.max(a) <= hi): bad.append("range of " + k)
        if np.any(a != np.floor(a)): bad.append("whole numbers in " + k)
    return bad
def pick(X, n):
    return np.take_along_axis(X, n.reshape(N, 8, 1, 16 * L), 3).reshape(N, 8, 16, 16, L)
def reference(clk, ttab, trav, last, slot):
    X = clk.astype(np.float32).astype(np.int32).reshape(N, 8, 16, W); TT = ttab.astype(np.int32).reshape(N, 8, 16, B)
    T = trav.astype(np.int32).reshape(N, 8, 16, L); c = last.astype(np.float32).astype(np.int32).reshape(N, 8, 16, L)
    b = np.stack([gentries(a) for a in slot]).astype(np.int32)
    bound = np.full((N, 8), 9, np.int32); row = np.arange(16, dtype=np.int32)[None, None, :, None]; lane = np.arange(L, dtype=np.int32)
    for v in range(RO):
        if v > 0:
            T = np.roll(T, ST, axis=0); c = np.roll(c, ST, axis=0); b = np.roll(b, ST, axis=0)
        at = np.broadcast_to(b[:, :, None, :], (N, 8, 16, L))
        H = np.take_along_axis(TT, at, 3); x = pick(X, T); y = pick(X, H)
        take = np.sum(y >= x, axis=2) >= bound[:, :, None, None]
        T = np.where(take, H, T); z = np.where(take[:, :, None], y, x)
        m = np.min(z, axis=3); M = np.max(z, axis=3)
        free = m > c; c = m
        n = (((T * (2 * m + 1)) >> 3) + 613 * row + 37 * at) & (W - 1)
        e = pick(X, n)
        ready = free & (np.sum(e >= m[:, :, :, None], axis=2) >= 12)
        T = np.where(ready, n, T)
        score = np.where(ready, np.sum(np.abs(e - M[:, :, :, None]), axis=2), -1)
        best = np.argmax(score, axis=2)
        has = np.any(ready, axis=2)
        low = np.argmax(b[:, :, :, None] == b[:, :, None, :], axis=3)
        np.put_along_axis(TT, at, np.take_along_axis(T, np.broadcast_to(low[:, :, None, :], (N, 8, 16, L)), 3), 3)
        col = np.broadcast_to((S * lane + (np.sum(M, axis=2) & (S - 1)))[:, :, None, :], (N, 8, 16, L))
        np.put_along_axis(X, col, (np.take_along_axis(X, col, 3) + M) >> 1, 3)
        b = np.where(has, np.take_along_axis(n, best[:, :, None, :], 2)[:, :, 0] & (B - 1), (b + 97) & (B - 1)).astype(np.int32)
        bound = 9 + (np.sum(~has, axis=2) & 1)
    return {"yclk": X.reshape(N, 128, W).astype(np.float32).astype(BF), "yttab": TT.reshape(N, 128, B).astype(np.float32), "ytrav": T.reshape(N, 128, L).astype(np.float32),
            "ylast": c.reshape(N, 128, L).astype(np.float32).astype(BF), "yslot": np.stack([gtable(a) for a in b]).astype(np.float32)}

@@ -1,0 +1,725 @@
+import numpy as np
+from concourse.bass import DstId, RemoteDMATransfer
+from concourse.mybir import AluOpType as A, ActivationFunctionType as F
+
+CFG = dict(
+    PX=[0, 64, 128, 192, 256],
+    P1=[0, 128, 256],
+    P2=[0, 128, 256],
+    P3=[0, 128, 256],
+    P4=[0, 128, 256],
+    GC="otbj",
+    RS=0, S8=0,
+    NSQ=1,
+    G=64,
+    SEED=0, SLACK=150.0, FB=3, ITER=60, STEP=3000.0, POLISH=1200, TEMP=60.0, FREE=0.4, SEC=0.5, FAR=0.2, ALL=0.5,
+    PER=34000.0, OFF=None,
+)
+COST = dict(cyc=1.04, fv=60.0, fs=70.0, ga=1.56, sc=3.8, pe=0.55, fp=10.0, lx=120.0, ls=70.0,
+            rl=3000.0, rb=0.03, ri=900.0, dl=2000.0, db=0.005)
+NV, L, W, B = 5, 256, 4096, 1024
+f32, bf, i32, u16 = "float32", "bfloat16", "int32", "uint16"
+
+
+def sb(n, d):
+    return ("sbuf", [128] + (n if isinstance(n, list) else [n]), d)
+
+
+SCRATCH = {
+    "X": sb(W, bf), "X2": sb(W, bf), "tti": sb(B, i32), "tt": sb(B + L, f32), "tri": sb(L, i32), "sli": sb(16, i32),
+    "lst": sb(L, bf),
+    "Tf": sb(NV * L, f32), "Tu": sb(NV * L, u16), "ci": sb(NV * L, bf), "bu": sb(NV * 16, u16), "off": sb(NV * 16, u16),
+    "T2": sb(NV * L, f32), "T2u": sb(NV * L, u16), "co": sb(NV * L, bf), "bo": sb(NV * 16, u16), "oo": sb(NV * 16, u16),
+    "bI": sb(16, i32), "ys": sb(16, f32),
+    "x": sb(W, bf), "c1": sb(W, bf), "z": sb(W, bf), "mn": sb(W, bf), "mx": sb(W, bf),
+    "e": sb(W, bf), "ab": sb(W, bf), "sg": sb(W, bf),
+    "Hu": sb(L, u16), "D": sb(L, f32), "T1": sb(L, f32), "T1u": sb(L, u16), "rel": sb(L, bf), "prod": sb(L, f32),
+    "qI": sb(L, i32), "nI": sb(L, i32), "nu": sb(L, u16), "n10": sb(L, i32), "rdy": sb(L, bf),
+    "key": sb(L, f32), "kT": sb(L, f32), "ks": sb(L, f32), "kI": sb(32, i32), "kA": sb(32, i32), "klo": sb(16, f32),
+    "w": sb(16, f32), "FB": sb(16, f32), "wI": sb(16, i32), "nh": sb(L, bf),
+    "r1": sb(8, f32), "r2": sb(8, f32), "bnd": sb(8, f32),
+    "brow": sb(L, f32), "CLi": sb(32, i32), "CL": sb(32, u16), "E": sb(2 * L, bf),
+    "o1": sb(16, f32), "o2": sb(16, f32),
+    "uI": sb(16, i32), "uA": sb(16, i32), "jI": sb(16, i32), "ju": sb(16, u16), "s8": sb(L, f32), "s8i": sb(L, i32),
+    "s8b": sb(L, bf), "xj": sb(L, bf), "neg": sb(L, bf),
+    "pI": sb(8, i32), "col": sb(16, f32), "J": sb(160, f32), "Jg": sb(128, f32), "Jr": sb([16, 8], f32),
+    "Jh": sb([16, 8], f32), "t1": sb([16, 8], bf), "t2": sb([16, 8], bf), "J16": sb(16, f32),
+    "IOT": sb(B, f32), "C4": sb(B, f32), "L16": sb(16, f32), "LD": sb(16, f32),
+    "I": sb(128, bf), "nId": sb(128, bf), "I16": sb(128, bf), "IK": sb(128, bf), "Ih": sb(128, bf),
+    "CKa": sb(128, bf), "CKb": sb(128, bf), "CK": sb(128, bf), "BO": sb(128, bf),
+    "W1": sb(144, bf), "W8": sb(144, bf), "Wh": sb(144, bf), "WI0": sb(160, f32), "WI1": sb(160, f32),
+    "SLT": sb([16, 144], bf), "rmin": sb(2048, bf), "rmax": sb(2048, bf), "rk": sb(L, bf), "ones": sb(128, bf),
+    "b0": ("psum", [128, 512], f32), "vp": ("psum", [128, 512], f32),
+    "d3": ("psum", [128, 512], f32), "d2": ("psum", [128, 512], f32),
+    "d0": ("psum", [128, 512], f32), "d1": ("psum", [128, 512], f32),
+    "kp": ("psum", [128, 512], f32), "b7": ("psum", [128, 512], f32),
+}
+BANKS = ("b0", "vp", "d3", "d0", "d1", "d2", "kp", "b7")
+SEMAPHORES = (["V", "S", "P", "G", "sent"] + ["dm%d" % i for i in range(16)]
+              + ["ar%d_%d_%d" % (v, c, k) for v in range(1, NV) for c in range(6) for k in range(3)]
+              + ["of%d" % v for v in range(1, NV)])
+
+
+def pieces(p):
+    return list(zip(p[:-1], p[1:]))[::-1]
+
+
+def build(g, T, dst, engines, cfg):
+    ops = []
+    V, S, P = g.vector, g.scalar, g.tensor
+
+    visit, seen = [-1], {}
+
+    def add(eng, fn, rd, wr, kind, n, extra=(), sem=None, cnt=0):
+        tag = (visit[0], eng, kind, (wr + rd)[0][0])
+        seen[tag] = seen.get(tag, 0) + 1
+        ops.append(dict(eng=eng, fn=fn, rd=rd, wr=wr, kind=kind, n=n, extra=list(extra), sem=sem, cnt=cnt, visit=visit[0],
+                        tag=(visit[0] < 0,) + tag[1:] + (seen[tag],)))
+        return len(ops) - 1
+
+    def vop(fn, rd, wr, n, m=1.0):
+        return add("V", fn, rd, wr, "v", max(64.0, n * m))
+
+    def ts(out, in0, s1, s2, o0, o1, rd, wr, n, m=1.0):
+        if o1 is None:
+            return vop(lambda: V.tensor_scalar(out, in0, s1, None, o0), rd, wr, n, m)
+        return vop(lambda: V.tensor_scalar(out, in0, s1, s2, o0, o1), rd, wr, n, m)
+
+    def tt(out, a, b, o, rd, wr, n, m=1.0):
+        return vop(lambda: V.tensor_tensor(out, a, b, o), rd, wr, n, m)
+
+    def cp(out, a, rd, wr, n, m=1.0):
+        return vop(lambda: V.tensor_copy(out, a), rd, wr, n, m)
+
+    def cvt(key, out, a, rd, wr, n):
+        if key in cfg["GC"]:
+            return add("G", lambda: g.affine_select(out, a, [[0, n]], A.is_ge, 0.0, 0, 0), rd, wr, "g", n)
+        return cp(out, a, rd, wr, n)
+
+    def ms(out, c, wr, n):
+        return vop(lambda: V.memset(out, c), [], wr, n, 0.5)
+
+    def gtt(out, a, b, o, rd, wr, n):
+        return add("V", lambda: V.tensor_tensor(out, a, b, o), rd, wr, "vg", n)
+
+    def gcp(out, a, rd, wr, n, kind="vg"):
+        return add("V", lambda: V.tensor_copy(out, a), rd, wr, kind, n)
+
+    def act(out, a, fn, bias, rd, wr, n, kind="s"):
+        if bias is None:
+            return add("S", lambda: S.activation(out, a, fn), rd, wr, kind, n)
+        return add("S", lambda: S.activation(out, a, fn, bias=bias), rd, wr, kind, n)
+
+    def mm(lst, rd, wr, f=1):
+        def go():
+            r = None
+            for o, l, rh, st, sp, n in lst:
+                r = P.matmul(o, l, rh, st, sp)
+            return r
+        return add("P", go, rd, wr, "p", (sum(max(64, t[5]) * f for t in lst), len(lst)))
+
+    ndma = [0]
+
+    def dma(q, out, a, rd, wr, nbytes):
+        e = g.sync if q == "Y" else g.scalar
+        ndma[0] += 1
+        return add(q, lambda: e.dma_start(out, a), rd, wr, "dma", nbytes, sem="dm%d" % (ndma[0] - 1), cnt=16)
+
+    def send(trs, rd):
+        def go():
+            if len(trs) == 1:
+                t = trs[0]
+                return g.remote_dma(t[1], t[0], T.sem[t[3]], T.sem["sent"], dst[1], dst[0], sum(1 << e for e in t[2]))
+            return g.remote_dma_fused([RemoteDMATransfer(dst_ids=[DstId(rid=dst[0], pnc=dst[1])],
+                                                         dma_engine_mask=sum(1 << e for e in t[2]),
+                                                         remote_sem=T.sem[t[3]], src=t[0], dst=t[1]) for t in trs],
+                                      local_sem=T.sem["sent"])
+        s = add("G", go, rd, [], "send", 0, cnt=sum(len(t[2]) for t in trs))
+        for name in sorted(set(t[3] for t in trs)):
+            mine = [t for t in trs if t[3] == name]
+            add(None, None, [], [r for t in mine for r in t[4]], "recv", sum(128 * t[5] for t in trs), extra=[s],
+                sem=name, cnt=sum(len(t[2]) for t in mine))
+
+    def al(n):
+        return (n, 0, 1 << 20)
+
+    def iota(out, pat, base, cm, wr, n, flt=True):
+        if flt:
+            return add("G", lambda: g.iota(out, pat, base, cm, allow_small_or_imprecise_dtypes=True), [], wr, "g", n)
+        return add("G", lambda: g.iota(out, pat, base, cm), [], wr, "g", n)
+
+    dma("Y", T["sli"][:], T.slot[:], [], [al("sli")], 8192)
+    dma("S", T["tri"][:], T.trav[:], [], [al("tri")], 131072)
+    dma("Y", T["X"][:], T.clk[:], [], [al("X")], 1048576)
+    dma("S", T["tti"][:], T.ttab[:], [], [al("tti")], 1572864)
+    dma("Y", T["lst"][:], T.last[:], [], [al("lst")], 1638400)
+
+    pI, col, J = T["pI"], T["col"], T["J"]
+    iota(pI[:, 0:1], [[1, 1]], 0, 1, [("pI", 0, 1)], 1, False)
+    iota(J[:], [[1, 160]], 0, 0, [al("J")], 160)
+    iota(T["J16"][:], [[16, 16]], 0, 0, [al("J16")], 16)
+    iota(T["IOT"][:], [[1, B]], 0, 0, [al("IOT")], B)
+    iota(T["Jr"][:], [[1, 16], [0, 8]], 0, 0, [al("Jr")], 128)
+    iota(T["Jh"][:], [[0, 16], [1, 8]], 0, 0, [al("Jh")], 128)
+    iota(T["Jg"][:], [[1, 8], [0, 16]], 0, 0, [al("Jg")], 128)
+
+    def pc(k):
+        return pI[:, k:k + 1]
+
+    def cc(k):
+        return col[:, k:k + 1]
+
+    def rp(k):
+        return ("pI", k, k + 1)
+
+    def rc(k):
+        return ("col", k, k + 1)
+    ts(pc(1), pc(0), 15, None, A.bitwise_and, None, [rp(0)], [rp(1)], 1)
+    ts(pc(2), pc(0), 4, None, A.arith_shift_right, None, [rp(0)], [rp(2)], 1)
+    ts(pc(3), pc(0), 4, 1, A.arith_shift_right, A.bitwise_and, [rp(0)], [rp(3)], 1)
+    ts(pc(4), pc(0), 7, None, A.bitwise_and, None, [rp(0)], [rp(4)], 1)
+    cp(col[:, 0:5], pI[:, 0:5], [("pI", 0, 5)], [("col", 0, 5)], 5)
+    ts(cc(5), cc(0), 16.0, None, A.add, None, [rc(0)], [rc(5)], 1)
+    ts(cc(6), cc(2), 16.0, 15.0, A.mult, A.add, [rc(2)], [rc(6)], 1)
+    ts(cc(7), cc(3), -1.0, 1.0, A.mult, A.add, [rc(3)], [rc(7)], 1)
+    ts(cc(8), cc(4), -1024.0, 15360.0, A.mult, A.add, [rc(4)], [rc(8)], 1)
+    ts(cc(9), cc(1), 2452.0, -0.25, A.mult, A.add, [rc(1)], [rc(9)], 1)
+    ts(cc(10), cc(1), 16.0 - 4 * cfg["NSQ"], -8.0, A.is_ge, A.mult, [rc(1)], [rc(10)], 1)
+    ts(cc(11), cc(10), 20.0 if cfg["RS"] else 28.0, None, A.add, None, [rc(10)], [rc(11)], 1)
+    ts(cc(12), cc(0), -1.0, 127.0, A.mult, A.add, [rc(0)], [rc(12)], 1)
+    for name, f in (("I", 1.0), ("nId", -1.0), ("I16", 8.0 if cfg["RS"] else 16.0), ("IK", 3.0 * 2 ** 24), ("Ih", 0.5)):
+        ts(T[name][:], J[:, 0:128], cc(0), f, A.is_equal, A.mult, [al("J"), rc(0)], [al(name)], 128)
+    ts(T["CKa"][:], J[:, 0:128], cc(0), cc(8), A.is_equal, A.mult, [al("J"), rc(0), rc(8)], [al("CKa")], 128)
+    ts(T["CKb"][:], J[:, 0:128], cc(12), -2.0 ** 26, A.is_equal, A.mult, [al("J"), rc(12)], [al("CKb")], 128)
+    tt(T["CK"][:], T["CKa"][:], T["CKb"][:], A.add, [al("CKa"), al("CKb")], [al("CK")], 128, 2)
+    ts(T["BO"][:], T["Jg"][:], cc(2), 0.5, A.is_equal, A.mult, [al("Jg"), rc(2)], [al("BO")], 128)
+    for name, f in (("W1", 1.0), ("W8", 8192.0), ("Wh", 0.5)):
+        ts(T[name][:], J[:, 0:144], cc(6), f, A.is_equal, A.mult, [al("J"), rc(6)], [al(name)], 144)
+    ts(T["WI0"][:], J[:], cc(5), cc(7), A.is_equal, A.mult, [al("J"), rc(5), rc(7)], [al("WI0")], 160)
+    ts(T["WI1"][:], J[:], cc(5), cc(3), A.is_equal, A.mult, [al("J"), rc(5), rc(3)], [al("WI1")], 160)
+    iota(T["SLT"][:], [[0, 16], [0, 144]], 0, 0, [al("SLT")], 2304)
+    ts(T["t1"][:], T["Jr"][:], cc(1), 8192.0, A.is_gt, A.mult, [al("Jr"), rc(1)], [al("t1")], 128)
+    ts(T["t2"][:], T["Jh"][:], cc(2), None, A.is_equal, None, [al("Jh"), rc(2)], [al("t2")], 128)
+    tt(T["SLT"][:, :, 15:143:16], T["t1"][:], T["t2"][:], A.mult, [al("t1"), al("t2")], [al("SLT")], 128, 2)
+    nsc = 16 * max(b - a for a, b in pieces(cfg["P2"]))
+    iota(T["rmin"][:, 0:nsc], [[0, nsc // 16], [-256, 16]], 255, 0, [al("rmin")], nsc)
+    iota(T["rmax"][:, 0:nsc], [[0, nsc // 16], [256, 16]], 0, 0, [al("rmax")], nsc)
+    ms(T["rk"][:], 0.0, [al("rk")], L)
+    ms(T["rk"][:, 0:L:8], -2.0 ** 28, [al("rk")], 32)
+    ms(T["ones"][:], 1.0, [al("ones")], 128)
+    if cfg["S8"]:
+        ms(T["neg"][:], -1.0, [al("neg")], L)
+    iota(T["CLi"][:, 0:16], [[1, 16]], 0, 0, [("CLi", 0, 16)], 16, False)
+    iota(T["CLi"][:, 16:32], [[2, 8], [0, 2]], 0, 0, [("CLi", 16, 32)], 16, False)
+    cp(T["CL"][:], T["CLi"][:], [al("CLi")], [al("CL")], 32)
+    ms(T["bnd"][:, 0:1], 0.0, [("bnd", 0, 1)], 1)
+    add("S", lambda: S.activation(T["C4"][:], T["IOT"][:], F.Identity, bias=cc(9), scale=148.0), [al("IOT"), rc(9)],
+        [al("C4")], "s", B)
+    ts(T["LD"][:], T["J16"][:], cc(1), float(B), A.add, A.add, [al("J16"), rc(1)], [al("LD")], 16)
+    ts(T["L16"][:], T["J16"][:], cc(1), 16.0, A.add, A.mult, [al("J16"), rc(1)], [al("L16")], 16)
+    cp(T["bu"][:, 0:16], T["sli"][:], [al("sli")], [("bu", 0, 16)], 16)
+    cp(T["Tu"][:, 0:L], T["tri"][:], [al("tri")], [("Tu", 0, L)], L)
+    cp(T["Tf"][:, 0:L], T["tri"][:], [al("tri")], [("Tf", 0, L)], L)
+    cp(T["tt"][:, 0:B], T["tti"][:], [al("tti")], [("tt", 0, B)], B)
+    ts(T["ci"][:, 0:L], T["lst"][:], 1.0, None, A.add, None, [al("lst")], [("ci", 0, L)], L, 0.5)
+
+    def sel(name, k):
+        return T[name][:, 15 - k:143 - k]
+
+    def lowest(lu, rlu, src, rsrc, out, rout):
+        E, b7 = T["E"], T["b7"]
+        act(T["brow"][:], T["IOT"][:, 0:B].indirect(lu), F.Copy, None, [al("IOT"), rlu], [al("brow")], L, "sg")
+        for k in range(2):
+            gtt(E[:, k * L:(k + 1) * L], src.indirect(T["CL"][:, 16 * k:16 * k + 16]), T["brow"][:], A.is_equal,
+                [rsrc, al("CL"), al("brow")], [("E", k, k + 1)], L)
+        mm([(b7[:, L:L + 16], T["SLT"][:, r, 15 - r:143 - r], E[:, r:L:16], r == 0, False, 16) for r in range(16)]
+           + [(b7[:, L + 1:L + 16:2], sel("W8", r), E[:, L + 16 + r:2 * L:32], False, r == 15, 8) for r in range(16)],
+           [al("E"), al("SLT"), al("W8")], [("b7", L, L + 16)])
+        tt(T["o1"][:], b7[:, L:L + 16], T["LD"][:], A.min, [("b7", L, L + 16), al("LD")], [al("o1")], 16)
+        tt(T["o2"][:], T["o1"][:], src, A.max, [al("o1"), rsrc], [al("o2")], 16)
+        cvt("o", out, T["o2"][:], [al("o2")], [rout], 16)
+
+    lowest(T["bu"][:, 0:16], ("bu", 0, 16), T["sli"][:], al("sli"), T["off"][:, 0:16], ("off", 0, 16))
+
+    X, tab, vp, b0, b7, kp = T["X"], T["tt"], T["vp"], T["b0"], T["b7"], T["kp"]
+    e, ap, mn, mx = T["e"], T["b7"], T["mn"], T["mx"]
+    dturn = [0]
+
+    def cut(a, b):
+        return [(s, min(b, s + cfg["G"])) for s in range(a, b, cfg["G"])]
+    for v in range(NV):
+        visit[0] = v
+        last = v == NV - 1
+        o, ob = v * L, v * 16
+        if last:
+            dma("Y", T["X2"][:], X[:], [al("X")], [al("X2")], 1048576)
+        for a, b in pieces(cfg["PX"]):
+            act(T["x"][:, 16 * a:16 * b], X[:, 0:W].indirect(T["Tu"][:, o + a:o + b]), F.Copy, None,
+                [al("X"), ("Tu", o + a, o + b)], [("x", a, b)], 16 * (b - a), "sg")
+        for a, b in pieces(cfg["P1"]):
+            n = b - a
+            bl, rbl = T["bu"][:, ob + a // 16:ob + b // 16], ("bu", ob + a // 16, ob + b // 16)
+            Tf, rT = T["Tf"][:, o + a:o + b], ("Tf", o + a, o + b)
+            tn = "tt" if v else "tti"
+            gcp(T["Hu"][:, a:b], T[tn][:, 0:B].indirect(bl), [al(tn), rbl], [("Hu", a, b)], n)
+            gtt(T["D"][:, a:b], T[tn][:, 0:B].indirect(bl), Tf, A.subtract, [al(tn), rbl, rT], [("D", a, b)], n)
+            for a2, b2 in cut(a, b):
+                gtt(T["c1"][:, 16 * a2:16 * b2], X[:, 0:W].indirect(T["Hu"][:, a2:b2]), T["x"][:, 16 * a2:16 * b2], A.is_ge,
+                    [al("X"), ("Hu", a2, b2), ("x", a2, b2)], [("c1", a2, b2)], 16 * (b2 - a2))
+            mm([(b0[:, a:b], sel("W1", k), T["c1"][:, 16 * a + k:16 * b:16], k == 0, k == 15, n) for k in range(16)],
+               [("c1", a, b), al("W1")], [("b0", a, b)])
+            ts(vp[:, a:b], b0[:, a:b], T["bnd"][:, v:v + 1], 9.0, A.subtract, A.is_ge, [("b0", a, b), ("bnd", v, v + 1)],
+               [("vp", a, b)], n)
+            tt(vp[:, a:b], vp[:, a:b], T["D"][:, a:b], A.mult, [("vp", a, b), ("D", a, b)], [("vp", a, b)], n)
+            tt(T["T1"][:, a:b], vp[:, a:b], Tf, A.add, [("vp", a, b), rT], [("T1", a, b)], n)
+            cp(T["T1u"][:, a:b], T["T1"][:, a:b], [("T1", a, b)], [("T1u", a, b)], n)
+            for a2, b2 in cut(a, b):
+                act(T["z"][:, 16 * a2:16 * b2], X[:, 0:W].indirect(T["T1u"][:, a2:b2]), F.Copy, None,
+                    [al("X"), ("T1u", a2, b2)], [("z", a2, b2)], 16 * (b2 - a2), "sg")
+        for a, b in pieces(cfg["P2"]):
+            n = b - a
+            zz = T["z"][:, 16 * a:16 * b]
+            vop(lambda a=a, b=b, n=n, zz=zz: V.tensor_tensor_scan(mn[:, 16 * a:16 * b], T["rmin"][:, 0:16 * n], zz, 0.0, A.max, A.min),
+                [("z", a, b), al("rmin")], [("mn", a, b)], 16 * n, 0.5)
+            vop(lambda a=a, b=b, n=n, zz=zz: V.tensor_tensor_scan(mx[:, 16 * a:16 * b], T["rmax"][:, 0:16 * n], zz, 0.0, A.min, A.max),
+                [("z", a, b), al("rmax")], [("mx", a, b)], 16 * n, 0.5)
+            m = mn[:, 16 * a + 15:16 * b:16]
+            ra = ("b7", a, b)
+            mm([(ap[:, a:b], T["I"][:], m, True, False, n), (ap[:, a:b], T["Ih"][:], T["ones"][:, 0:n], False, True, n)],
+               [("mn", a, b), al("I"), al("Ih"), al("ones")], [ra])
+            act(T["co"][:, o + a:o + b], m, F.Identity, 0.0 if last else 1.0, [("mn", a, b)], [("co", o + a, o + b)], n)
+            tt(T["prod"][:, a:b], ap[:, a:b], T["T1"][:, a:b], A.mult, [ra, ("T1", a, b)], [("prod", a, b)], n)
+            gtt(T["qI"][:, a:b], T["C4"][:, 0:B].indirect(T["bu"][:, ob + a // 16:ob + b // 16]), T["prod"][:, a:b], A.add,
+                [al("C4"), ("bu", ob + a // 16, ob + b // 16), ("prod", a, b)], [("qI", a, b)], n)
+            ts(T["nI"][:, a:b], T["qI"][:, a:b], 2, W - 1, A.arith_shift_right, A.bitwise_and, [("qI", a, b)], [("nI", a, b)], n)
+            cp(T["nu"][:, a:b], T["nI"][:, a:b], [("nI", a, b)], [("nu", a, b)], n)
+            if cfg["RS"]:
+                dn = "d%d" % (dturn[0] % 4)
+                dturn[0] += 1
+                mm([(T[dn][:, 0:n], T["I"][:], m, True, False, n),
+                    (T[dn][:, 0:n], T["nId"][:], T["ci"][:, o + a:o + b], False, True, n)],
+                   [("mn", a, b), ("ci", o + a, o + b), al("I"), al("nId")], [al(dn)])
+                act(T["rel"][:, a:b], T[dn][:, 0:n], F.Sign, 0.5, [al(dn)], [("rel", a, b)], n)
+            else:
+                tt(T["rel"][:, a:b], ap[:, a:b], T["ci"][:, o + a:o + b], A.is_gt, [ra, ("ci", o + a, o + b)],
+                   [("rel", a, b)], n)
+            ts(T["n10"][:, a:b], T["qI"][:, a:b], 2, B - 1, A.arith_shift_right, A.bitwise_and, [("qI", a, b)], [("n10", a, b)], n)
+            tt(vp[:, L + a:L + b], T["nI"][:, a:b], T["T1"][:, a:b], A.subtract, [("nI", a, b), ("T1", a, b)],
+               [("vp", L + a, L + b)], n, 2)
+        if last:
+            dma("Y", T.ylast[:], T["co"][:, o:o + L], [("co", o, o + L)], [], 65536)
+        mm([(b7[:, 272:288], sel("W1", r), mx[:, 16 * r + 15:W:256], r == 0, r == 15, 16) for r in range(16)],
+           [al("mx"), al("W1")], [("b7", 272, 288)])
+        cp(T["uI"][:], b7[:, 272:288], [("b7", 272, 288)], [al("uI")], 16)
+        ts(T["uA"][:], T["uI"][:], 15, None, A.bitwise_and, None, [al("uI")], [al("uA")], 16)
+        tt(T["jI"][:], T["uA"][:], T["L16"][:], A.add, [al("uA"), al("L16")], [al("jI")], 16)
+        cvt("j", T["ju"][:], T["jI"][:], [al("jI")], [al("ju")], 16)
+        if cfg["S8"]:
+            s8 = T["s8b"]
+            act(T["xj"][:], X[:, 0:W].indirect(T["ju"][:]), F.Copy, None, [al("X"), al("ju")], [al("xj")], L, "sg")
+            mm([(b0[:, 0:L], T["I"][:], T["xj"][:], True, False, L), (b0[:, 0:L], T["I"][:], mx[:, 15:W:16], False, False, L),
+                (b0[:, 0:L], T["Ih"][:], T["neg"][:], False, True, L)], [al("xj"), al("mx"), al("I"), al("Ih"), al("neg")],
+               [("b0", 0, L)])
+            add("S", lambda: S.activation(T["s8"][:], b0[:, 0:L], F.Identity, bias=1.5 * 2 ** 23, scale=0.5), [("b0", 0, L)],
+                [al("s8")], "s", L)
+            act(s8[:], T["s8"][:], F.Identity, -1.5 * 2 ** 23, [al("s8")], [al("s8i")], L)
+        else:
+            s8 = T["s8i"]
+            gtt(T["s8"][:], X[:, 0:W].indirect(T["ju"][:]), mx[:, 15:W:16], A.add, [al("X"), al("ju"), al("mx")], [al("s8")], L)
+            ts(s8[:], T["s8"][:], 0.5, -0.25, A.mult, A.add, [al("s8")], [al("s8i")], L)
+        if last:
+            gcp(T["X2"][:, 0:W].indirect(T["ju"][:]), s8[:], [al("s8i"), al("ju")], [al("X2")], L, "vs")
+            dma("Y", T.yclk[:], T["X2"][:], [al("X2")], [], 1048576)
+        ts(T["FB"][:], T["bu"][:, ob:ob + 16], 97.0 - 2 ** 24, None, A.add, None, [("bu", ob, ob + 16)], [al("FB")], 16)
+        for ch, (a, b) in enumerate(pieces(cfg["P3"])):
+            n = b - a
+            for a2, b2 in cut(a, b):
+                act(e[:, 16 * a2:16 * b2], X[:, 0:W].indirect(T["nu"][:, a2:b2]), F.Identity, 1.0, [al("X"), ("nu", a2, b2)],
+                    [("e", a2, b2)], 16 * (b2 - a2), "sg")
+            M, m = mx[:, 16 * a + 15:16 * b:16], mn[:, 16 * a + 15:16 * b:16]
+
+            def diff(q, y, ry, fn, bias, out):
+                dn = "d%d" % (dturn[0] % 4)
+                dturn[0] += 1
+                lst = []
+                for r in range(4):
+                    lst += [(T[dn][:, r * n:(r + 1) * n], T["I"][:], e[:, 16 * a + 4 * q + r:16 * b:16], True, False, n),
+                            (T[dn][:, r * n:(r + 1) * n], T["nId"][:], y, False, True, n)]
+                mm(lst, [("e", a, b), ry, al("I"), al("nId")], [al(dn)])
+                s0 = 16 * a + 4 * q * n
+                act(T[out][:, s0:s0 + 4 * n], T[dn][:, 0:4 * n], fn, bias, [al(dn)], [(out, s0, s0 + 4 * n)], 4 * n)
+            lst = []
+            for q in range(4):
+                onv = q < 4 - cfg["NSQ"]
+                if not onv:
+                    diff(q, m, ("mn", a, b), F.Sign, -0.5, "sg")
+                for p in range(4 * q, 4 * q + 4):
+                    s0 = 16 * a + p * n
+                    if onv:
+                        tt(T["sg"][:, s0:s0 + n], e[:, 16 * a + p:16 * b:16], ap[:, a:b], A.is_gt,
+                           [("e", a, b), ("b7", a, b)], [("sg", s0, s0 + n)], n)
+                    lst.append((b0[:, L + a:L + b], sel("W1" if onv else "Wh", p), T["sg"][:, s0:s0 + n], p == 0, False, n))
+            lst.append((b0[:, L + a:L + b], T["I16"][:], T["rel"][:, a:b], False, True, n))
+            mm(lst, [("sg", 16 * a, 16 * b), ("rel", a, b), al("W1"), al("Wh"), al("I16")], [("b0", L + a, L + b)])
+            ts(T["rdy"][:, a:b], b0[:, L + a:L + b], cc(11), None, A.is_ge, None, [("b0", L + a, L + b), rc(11)], [("rdy", a, b)], n)
+            rv = ("vp", L + a, L + b)
+            tt(vp[:, L + a:L + b], vp[:, L + a:L + b], T["rdy"][:, a:b], A.mult, [rv, ("rdy", a, b)], [rv], n)
+            r2 = ("T2", o + a, o + b)
+            tt(T["T2"][:, o + a:o + b], vp[:, L + a:L + b], T["T1"][:, a:b], A.add, [rv, ("T1", a, b)], [r2], n)
+            if not last:
+                cvt("t", T["T2u"][:, o + a:o + b], T["T2"][:, o + a:o + b], [r2], [("T2u", o + a, o + b)], n)
+                h, d = (a + b) // 2, o + L
+                s0, s1 = "ar%d_%d_0" % (v + 1, ch), "ar%d_%d_1" % (v + 1, ch)
+                k = len(engines) // 4
+                es = [engines[i::4][:k] for i in range(4)]
+                send([(T["T2u"][:, o + a:o + b], T["Tu"][:, d + a:d + b], es[0], s0, [("Tu", d + a, d + b)], 2 * n),
+                      (T["T2"][:, o + a:o + h], T["Tf"][:, d + a:d + h], es[2], s1, [("Tf", d + a, d + h)], 2 * n),
+                      (T["T2"][:, o + h:o + b], T["Tf"][:, d + h:d + b], es[3], s1, [("Tf", d + h, d + b)], 2 * n),
+                      (T["co"][:, o + a:o + b], T["ci"][:, d + a:d + b], es[1], s1, [("ci", d + a, d + b)], 2 * n)],
+                     [r2, ("T2u", o + a, o + b), ("co", o + a, o + b)])
+            for a5 in range(b - 32, a - 1, -32):
+                gcp(tab[:, 0:B + L].indirect(T["off"][:, ob + a5 // 16:ob + a5 // 16 + 2]), T["T2"][:, o + a5:o + a5 + 32],
+                    [r2, ("off", ob, ob + 16)], [al("tt")], 32, "vs")
+            for q in range(4):
+                diff(q, M, ("mx", a, b), F.Abs, -1.0, "ab")
+                mm([(kp[:, a:b], sel("W8", p), T["ab"][:, 16 * a + p * n:16 * a + (p + 1) * n], p == 0, False, n)
+                    for p in range(4 * q, 4 * q + 4)],
+                   [("ab", 16 * a + 4 * q * n, 16 * a + 4 * (q + 1) * n), al("W8")], [("kp", a, b), al("kgrp")])
+            mm([(kp[:, a:b], T["CK"][:], T["ones"][:, 0:n], False, False, n), (kp[:, a:b], T["IK"][:], T["rdy"][:, a:b], False, True, n)],
+               [("rdy", a, b), al("CK"), al("IK"), al("ones")], [("kp", a, b), al("kgrp")])
+            if a not in cfg["P4"]:
+                continue
+            ch = cfg["P4"].index(a)
+            b = cfg["P4"][ch + 1]
+            n = b - a
+            tt(T["key"][:, a:b], kp[:, a:b], T["n10"][:, a:b], A.add, [("kp", a, b), ("n10", a, b)], [("key", a, b)], n)
+            vop(lambda a=a, b=b: V.transpose(T["kT"][:, a:b], T["key"][:, a:b]), [("key", a, b)], [("kT", a, b)], n)
+            vop(lambda a=a, b=b, n=n: V.tensor_tensor_scan(T["ks"][:, a:b], T["rk"][:, 0:n], T["kT"][:, a:b], 0.0, A.add, A.max),
+                [("kT", a, b), al("rk")], [("ks", a, b)], n)
+            a8, b8, a6, b6 = a // 8, b // 8, a // 16, b // 16
+            cp(T["kI"][:, a8:b8], T["ks"][:, a + 7:b:8], [("ks", a, b)], [("kI", a, b)], 16)
+            ts(T["kA"][:, a8:b8], T["kI"][:, a8:b8], -7169, None, A.bitwise_and, None, [("kI", a, b)], [("kA", a, b)], 16)
+            ts(T["klo"][:, a6:b6], T["kA"][:, a8:b8:2], 1024.0, None, A.add, None, [("kA", a, b)], [("klo", a, b)], 16)
+            tt(T["w"][:, a6:b6], T["klo"][:, a6:b6], T["kA"][:, a8 + 1:b8:2], A.max, [("kA", a, b), ("klo", a, b)], [("w", a, b)], 16)
+            lst = []
+            for u in range(2):
+                for h in range(2):
+                    s0 = 16 - 16 * (h - u)
+                    lst.append((b7[:, 288 + a6 + u:288 + b6:2], T["WI%d" % u][:, s0:s0 + 128], T["w"][:, a6 + h:b6:2],
+                                h == 0, h == 1, 8))
+            rw = ("b7", 288 + a6, 288 + b6)
+            mm(lst, [("w", a, b), al("WI0"), al("WI1")], [rw], 4)
+            tt(T["wI"][:, a6:b6], b7[:, 288 + a6:288 + b6], T["FB"][:, a6:b6], A.max, [rw, al("FB")], [("wI", a, b)], 16)
+            ts(T["bI"][:, a6:b6], T["wI"][:, a6:b6], B - 1, None, A.bitwise_and, None, [("wI", a, b)], [("bI", a, b)], 16)
+            if last:
+                cp(T["ys"][:, a6:b6], T["bI"][:, a6:b6], [("bI", a, b)], [("ys", a, b)], 16)
+            else:
+                rb = ("bo", ob + a6, ob + b6)
+                cvt("b", T["bo"][:, ob + a6:ob + b6], T["bI"][:, a6:b6], [("bI", a, b)], [rb], b6 - a6)
+                send([(T["bo"][:, ob + a6:ob + b6], T["bu"][:, ob + 16 + a6:ob + 16 + b6], engines, "ar%d_%d_2" % (v + 1, ch),
+                       [("bu", ob + 16 + a6, ob + 16 + b6)], n // 8)], [rb])
+        if last:
+            dma("Y", T.yttab[:], tab[:, 0:B], [al("tt")], [], 524288)
+            dma("Y", T.ytrav[:], T["T2"][:, o:o + L], [("T2", o, o + L)], [], 131072)
+            dma("Y", T.yslot[:], T["ys"][:], [al("ys")], [], 8192)
+            break
+        gcp(X[:, 0:W].indirect(T["ju"][:]), s8[:], [al("s8i"), al("ju")], [al("X")], L, "vs")
+        mm([(b0[:, 0:L], T["BO"][:], T["rdy"][:], True, True, L)], [al("rdy"), al("BO")], [("b0", 0, L)])
+        add("S", lambda: S.activation(T["nh"][:], b0[:, 0:L], F.Sign, accum_out=T["r1"][:, 0:1]), [("b0", 0, L)],
+            [al("r1"), al("nh")], "s", L + 140)
+        ts(T["r2"][:, 0:1], T["r1"][:, 0:1], 1.5 * 2 ** 24, -1.5 * 2 ** 24, A.add, A.add, [al("r1")], [al("r2")], 1)
+        tt(T["bnd"][:, v + 1:v + 2], T["r1"][:, 0:1], T["r2"][:, 0:1], A.not_equal, [al("r1"), al("r2")], [("bnd", v + 1, v + 2)], 1)
+        lowest(T["bo"][:, ob:ob + 16], ("bo", ob, ob + 16), T["bI"][:], al("bI"), T["oo"][:, ob:ob + 16], ("oo", ob, ob + 16))
+        send([(T["oo"][:, ob:ob + 16], T["off"][:, ob + 16:ob + 32], engines, "of%d" % (v + 1), [("off", ob + 16, ob + 32)], 32)],
+             [("oo", ob, ob + 16)])
+    return ops
+
+
+def data_deps(ops):
+    hist, deps = {}, []
+    for i, op in enumerate(ops):
+        d = set(op["extra"])
+        for name, lo, hi in op["rd"]:
+            d.update(j for j, l2, h2, wr in hist.get(name, ()) if wr and l2 < hi and lo < h2)
+        for name, lo, hi in op["wr"]:
+            d.update(j for j, l2, h2, wr in hist.get(name, ()) if l2 < hi and lo < h2)
+        d.discard(i)
+        deps.append(d)
+        for name, lo, hi in op["rd"]:
+            hist.setdefault(name, []).append((i, lo, hi, False))
+        for name, lo, hi in op["wr"]:
+            hist[name] = [t for t in hist.get(name, []) if not (lo <= t[1] and t[2] <= hi)] + [(i, lo, hi, True)]
+    return deps
+
+
+def costs(ops, c):
+    out = []
+    for op in ops:
+        k, n = op["kind"], op["n"]
+        if k == "dma":
+            out.append((100.0, c["dl"] + n * c["db"]))
+        elif k == "send":
+            out.append((c["ri"], c["ri"]))
+        elif k == "recv":
+            out.append((0.0, c["rl"] - c["ri"] + n * c["rb"]))
+        else:
+            if k == "p":
+                t = n[0] * c["pe"] + n[1] * c["fp"]
+            elif k == "g":
+                t = 150.0 + 2 * n * c["cyc"]
+            else:
+                t = (c["fv"] if op["eng"] == "V" else c["fs"]) + n * c["cyc"] * (c["ga"] if k[1:] == "g" else c["sc"] if k == "vs" else 1.0)
+            out.append((t, t))
+    return out
+
+
+def tag_numbers(ops):
+    num = {}
+    return [num.setdefault(op["tag"], len(num)) for op in ops]
+
+
+def priorities(ops, tags, off, cfg):
+    return [-(max(op["visit"], 0) * cfg["PER"] + 10.0 * off[t]) for op, t in zip(ops, tags)]
+
+
+def schedule(ops, deps, cfg, c, seed):
+    n = len(ops)
+    cs = costs(ops, c)
+    succ = [set() for _ in range(n)]
+    for i in range(n):
+        for j in deps[i]:
+            succ[j].add(i)
+    prio = [0.0] * n
+    for i in range(n - 1, -1, -1):
+        prio[i] = cs[i][1] + max([prio[j] + c["lx"] for j in succ[i]] + [0.0])
+    banks = [sorted(set(r[0] for r in op["rd"] + op["wr"] if r[0] in BANKS)) for op in ops]
+    rng = np.random.default_rng(seed)
+    if cfg["OFF"]:
+        r = one_pass(ops, deps, succ, cs, priorities(ops, tag_numbers(ops), cfg["OFF"], cfg), cfg, c, banks)
+        return polish(ops, deps, succ, cs, banks, r[1], cfg, c, rng)
+    best = None
+    for k in range(cfg["FB"] + 1):
+        r = one_pass(ops, deps, succ, cs, prio, cfg, c, banks)
+        if best is None or r[0] < best[0]:
+            best, bprio = r, prio
+        if k < cfg["FB"]:
+            prio = one_pass(ops, succ, deps, cs, r[3], cfg, c, banks)[3]
+    tags = {}
+    for i, op in enumerate(ops):
+        if op["eng"]:
+            tags.setdefault(op["tag"], []).append(i)
+    groups = list(tags.values())
+    cur, cprio = best[0], bprio
+    for k in range(cfg["ITER"]):
+        prio = list(cprio)
+        if k % 4 == 3:
+            fin = one_pass(ops, deps, succ, cs, prio, cfg, c, banks)[3]
+            amp = float(rng.random()) * cfg["STEP"] / 2
+            prio = one_pass(ops, succ, deps, cs, [f + float(x) * amp for f, x in zip(fin, rng.random(n))], cfg, c, banks)[3]
+        for t in rng.integers(0, len(groups), int(rng.integers(1, 4))):
+            s = float(rng.normal()) * cfg["STEP"]
+            one = int(rng.integers(0, 12))
+            for i in (groups[t][one:one + 1] if one < len(groups[t]) else groups[t]):
+                prio[i] += s
+        r = one_pass(ops, deps, succ, cs, prio, cfg, c, banks)
+        if r[0] <= cur + 600.0 * (1.0 - k / cfg["ITER"]) * float(rng.random()):
+            cur, cprio = r[0], prio
+        if r[0] < best[0]:
+            best = r
+    return polish(ops, deps, succ, cs, banks, best[1], cfg, c, rng)
+
+
+def polish(ops, deps, succ, cs, banks, order, cfg, c, rng):
+    n = len(ops)
+    eng = [op["eng"] for op in ops]
+    dl = [[(j, (0.0 if eng[i] == "P" else c["ls"]) if eng[i] == eng[j] and ops[j]["kind"] != "dma" else c["lx"])
+           for j in deps[i]] for i in range(n)]
+    where = {(op["visit"], op["tag"]): i for i, op in enumerate(ops)}
+    lx = c["lx"]
+
+    def run(order):
+        free, users, fin, why = {}, {bk: {} for bk in BANKS}, [0.0] * n, [-1] * n
+        for i in order:
+            en = eng[i]
+            t, w = free.get(en, (0.0, -1))
+            for j, l in dl[i]:
+                if fin[j] + l > t:
+                    t, w = fin[j] + l, j
+            for bk in banks[i]:
+                u = users[bk]
+                for e2, j in u.items():
+                    if e2 != en and fin[j] + lx > t:
+                        t, w = fin[j] + lx, j
+                u[en] = i
+            fin[i], why[i] = t + cs[i][1], w
+            if en:
+                free[en] = (t + cs[i][0], i)
+        return max(fin) + cfg["SEC"] * sum(fin) / n, fin, why
+
+    def move(order, u, v, ahead):
+        a, b = order.index(u), order.index(v)
+        if a >= b:
+            return order
+        mid = order[a:b + 1]
+        if ahead:
+            take = {v}
+            for i in mid[::-1]:
+                if i in take or not take.isdisjoint(succ[i]):
+                    take.add(i)
+            if u in take:
+                return order
+            return order[:a] + [i for i in mid if i in take] + [i for i in mid if i not in take] + order[b + 1:]
+        take = {u}
+        for i in mid:
+            if i in take or not take.isdisjoint(deps[i]):
+                take.add(i)
+        if v in take:
+            return order
+        return order[:a] + [i for i in mid if i not in take] + [i for i in mid if i in take] + order[b + 1:]
+    cur = run(order)
+    best = (cur[0], order)
+    for k in range(cfg["POLISH"]):
+        i = cur[1].index(max(cur[1]))
+        arcs = []
+        while cur[2][i] >= 0:
+            if cur[2][i] not in deps[i]:
+                arcs.append((cur[2][i], i))
+            i = cur[2][i]
+        if not arcs:
+            break
+        s = int(rng.integers(0, len(arcs)))
+        u, v = arcs[s]
+        for _ in range(int(rng.integers(0, 4))):
+            if s + 1 < len(arcs) and arcs[s + 1][1] == u:
+                s += 1
+                u = arcs[s][0]
+        if rng.random() < cfg["FREE"]:
+            s = int(rng.integers(1, n))
+            v = order[s]
+            mates = [i for i in order[max(0, s - 60):s] if eng[i] == eng[v]]
+            if not eng[v] or not mates:
+                continue
+            u = mates[-1 - int(rng.integers(0, min(len(mates), 12)))]
+            if rng.random() < cfg["FAR"]:
+                u = order[max(0, s - int(rng.integers(1, 120)))]
+        ahead, new = rng.random() < 0.5, order
+        shifts = range(-NV, NV) if rng.random() < cfg["ALL"] and min(ops[u]["visit"], ops[v]["visit"]) >= 0 else [0]
+        for d in shifts:
+            u2, v2 = where.get((ops[u]["visit"] + d, ops[u]["tag"])), where.get((ops[v]["visit"] + d, ops[v]["tag"]))
+            if u2 is not None and v2 is not None:
+                new = move(new, u2, v2, ahead)
+        r = run(new)
+        if r[0] <= cur[0] - cfg["TEMP"] * (1.0 - k / cfg["POLISH"]) * float(np.log(rng.random() + 1e-12)):
+            cur, order = r, new
+            if r[0] < best[0]:
+                best = (r[0], new)
+    users, alld = {bk: {} for bk in BANKS}, [None] * n
+    for i in best[1]:
+        alld[i] = set(deps[i])
+        for bk in banks[i]:
+            alld[i].update(j for e2, j in users[bk].items() if e2 != eng[i])
+            users[bk][eng[i]] = i
+    return best[0], best[1], alld
+
+
+def one_pass(ops, deps, succ, cs, prio, cfg, c, banks):
+    n = len(ops)
+    left = [len(d) for d in deps]
+    ready = [i for i in range(n) if not left[i]]
+    free, fin, users, order, alld, base = {}, [0.0] * n, {}, [], [None] * n, [0.0] * n
+
+    def lat(i, j):
+        a, b = ops[i]["eng"], ops[j]["eng"]
+        if a == b and ops[j]["kind"] != "dma":
+            return 0.0 if a == "P" else c["ls"]
+        return c["lx"]
+    eng, lx, est = [op["eng"] for op in ops], c["lx"], [0.0] * n
+    while ready:
+        t0, i0 = 1e30, -1
+        for i in ready:
+            t, f = base[i], free.get(eng[i], 0.0)
+            if f > t:
+                t = f
+            for bk in banks[i]:
+                for en, j in users.get(bk, {}).items():
+                    if en != eng[i] and fin[j] + lx > t:
+                        t = fin[j] + lx
+            est[i] = t
+            if t < t0:
+                t0, i0 = t, i
+        i, e0, t0 = i0, eng[i0], t0 + cfg["SLACK"]
+        for k in ready:
+            if prio[k] > prio[i] and est[k] <= t0 and eng[k] == e0:
+                i = k
+        d = set(deps[i])
+        for bk in banks[i]:
+            d.update(j for en, j in users.get(bk, {}).items() if en != ops[i]["eng"])
+            users.setdefault(bk, {})[ops[i]["eng"]] = i
+        alld[i] = d
+        fin[i] = est[i] + cs[i][1]
+        if ops[i]["eng"]:
+            free[ops[i]["eng"]] = est[i] + cs[i][0]
+        order.append(i)
+        ready.remove(i)
+        for j in succ[i]:
+            left[j] -= 1
+            if not left[j]:
+                base[j] = max(fin[k] + lat(j, k) for k in deps[j])
+                ready.append(j)
+    return max(fin), order, alld, fin
+
+
+PLAN = {}
+
+
+def rank_program(g, core, T, topo):
+    rank = T.rank_of(core)
+    if rank is None:
+        return
+    nxt = T.cores[(rank + 1) % len(T.cores)]
+    ops = build(g, T, topo.addr(nxt)[:2], topo.engines(core, nxt), CFG)
+    if not PLAN:
+        deps = data_deps(ops)
+        PLAN["p"] = schedule(ops, deps, CFG, COST, CFG["SEED"])
+    order, deps = PLAN["p"][1:]
+    q = {"V": g.vector, "S": g.scalar, "P": g.tensor, "G": g, "Y": g.sync}
+    known = {k: {} for k in q}
+    count = {k: 0 for k in "VSPG"}
+    token, clock, sent, ends = {}, {}, 0, {}
+    for i in order:
+        op = ops[i]
+        en = op["eng"]
+        if en is None:
+            token[i], clock[i] = (op["sem"], op["cnt"]), {op["sem"]: op["cnt"]}
+            ends[op["sem"]] = op["cnt"]
+            continue
+        need = {}
+        for j in deps[i]:
+            if en == "P" and ops[j]["eng"] == "P":
+                continue
+            if j in token and token[j][1] > need.get(token[j][0], (0, 0))[0]:
+                need[token[j][0]] = (token[j][1], j)
+        kn = known[en]
+        for s, (val, j) in sorted(need.items(), key=lambda t: -len(clock[t[1][1]])):
+            if kn.get(s, 0) < val:
+                q[en].wait_ge(T.sem[s], val)
+                for s2, v2 in clock[j].items():
+                    kn[s2] = max(kn.get(s2, 0), v2)
+        r = op["fn"]()
+        if op["kind"] == "send":
+            sent += op["cnt"]
+            continue
+        if op["kind"] == "dma":
+            r.then_inc(T.sem[op["sem"]], 16)
+            token[i] = (op["sem"], 16)
+        else:
+            r.then_inc(T.sem[en], 1)
+            count[en] += 1
+            token[i] = (en, count[en])
+        ends[token[i][0]] = token[i][1]
+        clock[i] = dict(kn)
+        clock[i][token[i][0]] = token[i][1]
+    ends["sent"] = sent
+    for s, val in ends.items():
+        if known["G"].get(s, 0) < val:
+            g.wait_ge(T.sem[s], val)

@@ -4,18 +4,21 @@ from concourse.mybir import AluOpType as A, ActivationFunctionType as F
 
 CFG = dict(
     PX=[0, 64, 128, 192, 256],
-    P1=[0, 128, 256],
+    XV=[],
+    P1=[0, 64, 128, 192, 256],
     P2=[0, 128, 256],
     P3=[0, 128, 256],
+    PT=[0, 128, 256],
     P4=[0, 128, 256],
-    GC="otbj",
-    RS=0, S8=0,
-    NSQ=1,
+    CV="",
+    NSQ={0: 0, 128: 0},
+    WAW=0, S8=1, HS=1, FS=1,
+    SGAT={0: 0, 64: 0, 128: 2, 192: 0},
+    BK=128, PH=[0, 128, 256], PM=[0, 128, 256], PC=[0, 128, 256],
     G=64,
-    SEED=0, SLACK=150.0, FB=3, ITER=60, STEP=3000.0, POLISH=1200, TEMP=60.0, FREE=0.4, SEC=0.5, FAR=0.2, ALL=0.5,
-    PER=34000.0, OFF=None,
+    SEED=0, SLACK=150.0, FB=3, ITER=60, STEP=3000.0, POLISH=3000, ANNEAL=8000, TEMP=200.0, FREE=0.4, SEC=0.1, FAR=0.2, ALL=0.5,
 )
-COST = dict(cyc=1.04, fv=60.0, fs=70.0, ga=1.56, sc=3.8, pe=0.55, fp=10.0, lx=120.0, ls=70.0,
+COST = dict(cyc=1.0, fv=55.0, fs=70.0, ga=1.5, sc=3.8, pe=0.52, fp=10.0, lx=120.0, ls=70.0,
             rl=3000.0, rb=0.03, ri=900.0, dl=2000.0, db=0.005)
 NV, L, W, B = 5, 256, 4096, 1024
 f32, bf, i32, u16 = "float32", "bfloat16", "int32", "uint16"
@@ -26,52 +29,56 @@ def sb(n, d):
 
 
 SCRATCH = {
-    "X": sb(W, bf), "X2": sb(W, bf), "tti": sb(B, i32), "tt": sb(B + L, f32), "tri": sb(L, i32), "sli": sb(16, i32),
-    "lst": sb(L, bf),
-    "Tf": sb(NV * L, f32), "Tu": sb(NV * L, u16), "ci": sb(NV * L, bf), "bu": sb(NV * 16, u16), "off": sb(NV * 16, u16),
-    "T2": sb(NV * L, f32), "T2u": sb(NV * L, u16), "co": sb(NV * L, bf), "bo": sb(NV * 16, u16), "oo": sb(NV * 16, u16),
-    "bI": sb(16, i32), "ys": sb(16, f32),
+    "X0": sb(W + 16, bf), "X1": sb(W + 16, bf), "tti": sb(B, i32), "tt": sb(B + L, f32), "tri": sb(L, i32),
+    "sli": sb(16, i32),
+    "Tu": sb(NV * L, u16), "ci": sb(NV * L, bf), "bu": sb(NV * 16, u16),
+    "T2u": sb(NV * L, u16), "co": sb(NV * L, bf), "bo": sb(NV * 16, u16),
+    "Tf": sb(L, f32), "T2": sb(L, f32), "bI": sb(16, i32), "ys": sb(16, f32), "bfl": sb(16, f32), "sC": sb(16, f32),
+    "off": sb(16, u16),
     "x": sb(W, bf), "c1": sb(W, bf), "z": sb(W, bf), "mn": sb(W, bf), "mx": sb(W, bf),
     "e": sb(W, bf), "ab": sb(W, bf), "sg": sb(W, bf),
-    "Hu": sb(L, u16), "D": sb(L, f32), "T1": sb(L, f32), "T1u": sb(L, u16), "rel": sb(L, bf), "prod": sb(L, f32),
-    "qI": sb(L, i32), "nI": sb(L, i32), "nu": sb(L, u16), "n10": sb(L, i32), "rdy": sb(L, bf),
-    "key": sb(L, f32), "kT": sb(L, f32), "ks": sb(L, f32), "kI": sb(32, i32), "kA": sb(32, i32), "klo": sb(16, f32),
-    "w": sb(16, f32), "FB": sb(16, f32), "wI": sb(16, i32), "nh": sb(L, bf),
-    "r1": sb(8, f32), "r2": sb(8, f32), "bnd": sb(8, f32),
-    "brow": sb(L, f32), "CLi": sb(32, i32), "CL": sb(32, u16), "E": sb(2 * L, bf),
-    "o1": sb(16, f32), "o2": sb(16, f32),
+    "Hu": sb(L, u16), "Hf": sb(L, f32), "tk": sb(L, bf), "u": sb(L, f32), "T1u": sb(L, u16), "T1": sb(L, f32),
+    "qI": sb(L, i32), "nI": sb(L, i32), "nf": sb(L, f32), "nu": sb(L, u16), "hh": sb(L, bf), "nr": sb(L, bf),
+    "kT": sb(L, f32), "ks": sb(L, f32), "kI": sb(32, i32), "kA": sb(32, i32), "klo": sb(16, f32),
+    "w": sb(16, f32), "FB": sb(16, f32), "wI": sb(16, i32), "nh": sb(16, bf),
+    "r1": sb(8, f32), "r2": sb(8, bf), "bnd": sb(8, f32),
+    "brC": sb(L, f32), "CLi": sb(32, i32), "CL": sb(32, u16), "E": sb(2 * L, bf), "o1": sb(16, f32),
     "uI": sb(16, i32), "uA": sb(16, i32), "jI": sb(16, i32), "ju": sb(16, u16), "s8": sb(L, f32), "s8i": sb(L, i32),
-    "s8b": sb(L, bf), "xj": sb(L, bf), "neg": sb(L, bf),
-    "pI": sb(8, i32), "col": sb(16, f32), "J": sb(160, f32), "Jg": sb(128, f32), "Jr": sb([16, 8], f32),
+    "pI": sb(8, i32), "col": sb(24, f32), "J": sb(160, f32), "Jg": sb(128, f32), "Jr": sb([16, 8], f32),
     "Jh": sb([16, 8], f32), "t1": sb([16, 8], bf), "t2": sb([16, 8], bf), "J16": sb(16, f32),
     "IOT": sb(B, f32), "C4": sb(B, f32), "L16": sb(16, f32), "LD": sb(16, f32),
-    "I": sb(128, bf), "nId": sb(128, bf), "I16": sb(128, bf), "IK": sb(128, bf), "Ih": sb(128, bf),
-    "CKa": sb(128, bf), "CKb": sb(128, bf), "CK": sb(128, bf), "BO": sb(128, bf),
+    "I": sb(128, bf), "nI_": sb(128, bf), "Ih": sb(128, bf), "I16": sb(128, bf), "rel": sb(L, bf), "NH": sb(128, bf),
+    "NK": sb(128, bf), "If": sb(128, f32), "nIf": sb(128, f32),
+    "CKa": sb(128, bf), "CKb": sb(128, bf), "CK": sb(128, bf), "BO": sb(128, f32),
     "W1": sb(144, bf), "W8": sb(144, bf), "Wh": sb(144, bf), "WI0": sb(160, f32), "WI1": sb(160, f32),
     "SLT": sb([16, 144], bf), "rmin": sb(2048, bf), "rmax": sb(2048, bf), "rk": sb(L, bf), "ones": sb(128, bf),
-    "b0": ("psum", [128, 512], f32), "vp": ("psum", [128, 512], f32),
-    "d3": ("psum", [128, 512], f32), "d2": ("psum", [128, 512], f32),
-    "d0": ("psum", [128, 512], f32), "d1": ("psum", [128, 512], f32),
-    "kp": ("psum", [128, 512], f32), "b7": ("psum", [128, 512], f32),
+    "a0": ("psum", [128, 512], f32), "a1": ("psum", [128, 512], f32),
+    "a2": ("psum", [128, 512], f32), "kp": ("psum", [128, 512], f32), "ms": ("psum", [128, 512], f32),
+    "d0": ("psum", [128, 512], f32), "d1": ("psum", [128, 512], f32), "a3": ("psum", [128, 512], f32),
 }
-BANKS = ("b0", "vp", "d3", "d0", "d1", "d2", "kp", "b7")
-SEMAPHORES = (["V", "S", "P", "G", "sent"] + ["dm%d" % i for i in range(16)]
-              + ["ar%d_%d_%d" % (v, c, k) for v in range(1, NV) for c in range(6) for k in range(3)]
-              + ["of%d" % v for v in range(1, NV)])
+BANKS = ("a0", "a1", "a2", "kp", "ms", "d0", "d1", "a3")
+SEMAPHORES = (["V", "S", "P", "G", "sent"] + ["dm%d" % i for i in range(20)]
+              + ["%s%d_%d" % (k, v, c) for k in "tbc" for v in range(1, NV) for c in range(0, L, 32)])
 
 
 def pieces(p):
     return list(zip(p[:-1], p[1:]))[::-1]
 
 
+def classes(n):
+    return 4 if n > 64 else 2 if n > 32 else 1
+
+
 def build(g, T, dst, engines, cfg):
     ops = []
     V, S, P = g.vector, g.scalar, g.tensor
-
-    visit, seen = [-1], {}
+    mask = sum(1 << e for e in engines)
+    visit, seen, opened = [-1], {}, {}
+    BK = cfg["BK"]
+    DB = ["d0", "d1"] + (["a3"] if BK == 128 else [])
 
     def add(eng, fn, rd, wr, kind, n, extra=(), sem=None, cnt=0):
-        tag = (visit[0], eng, kind, (wr + rd)[0][0])
+        tag = (visit[0], eng, kind, (wr + rd)[0][0].rstrip("0123456789"))
         seen[tag] = seen.get(tag, 0) + 1
         ops.append(dict(eng=eng, fn=fn, rd=rd, wr=wr, kind=kind, n=n, extra=list(extra), sem=sem, cnt=cnt, visit=visit[0],
                         tag=(visit[0] < 0,) + tag[1:] + (seen[tag],)))
@@ -91,10 +98,11 @@ def build(g, T, dst, engines, cfg):
     def cp(out, a, rd, wr, n, m=1.0):
         return vop(lambda: V.tensor_copy(out, a), rd, wr, n, m)
 
+    def gc_(out, a, rd, wr, n):
+        return add("G", lambda: g.affine_select(out, a, [[0, n]], A.is_ge, 0.0, 0, 0), rd, wr, "g", n)
+
     def cvt(key, out, a, rd, wr, n):
-        if key in cfg["GC"]:
-            return add("G", lambda: g.affine_select(out, a, [[0, n]], A.is_ge, 0.0, 0, 0), rd, wr, "g", n)
-        return cp(out, a, rd, wr, n)
+        return (cp if key in cfg["CV"] else gc_)(out, a, rd, wr, n)
 
     def ms(out, c, wr, n):
         return vop(lambda: V.memset(out, c), [], wr, n, 0.5)
@@ -105,18 +113,23 @@ def build(g, T, dst, engines, cfg):
     def gcp(out, a, rd, wr, n, kind="vg"):
         return add("V", lambda: V.tensor_copy(out, a), rd, wr, kind, n)
 
-    def act(out, a, fn, bias, rd, wr, n, kind="s"):
-        if bias is None:
-            return add("S", lambda: S.activation(out, a, fn), rd, wr, kind, n)
-        return add("S", lambda: S.activation(out, a, fn, bias=bias), rd, wr, kind, n)
+    def act(out, a, fn, rd, wr, n, kind="s", **kw):
+        return add("S", lambda: S.activation(out, a, fn, **kw), rd, wr, kind, n)
 
-    def mm(lst, rd, wr, f=1):
+    def mm(lst, rd, wr, start=True):
+        stop = [True]
+
         def go():
             r = None
-            for o, l, rh, st, sp, n in lst:
-                r = P.matmul(o, l, rh, st, sp)
+            for k, t in enumerate(lst):
+                r = P.matmul(t[0], t[1], t[2], start and k == 0, stop[0] and k == len(lst) - 1)
             return r
-        return add("P", go, rd, wr, "p", (sum(max(64, t[5]) * f for t in lst), len(lst)))
+        i = add("P", go, rd, wr, "p", (sum(max(64, t[3]) * t[4] for t in lst), len(lst)))
+        bank = [r[0] for r in wr + rd if r[0] in BANKS][0]
+        if start:
+            opened[bank] = i
+        ops[i].update(stop=stop, group=opened[bank])
+        return i
 
     ndma = [0]
 
@@ -125,20 +138,10 @@ def build(g, T, dst, engines, cfg):
         ndma[0] += 1
         return add(q, lambda: e.dma_start(out, a), rd, wr, "dma", nbytes, sem="dm%d" % (ndma[0] - 1), cnt=16)
 
-    def send(trs, rd):
-        def go():
-            if len(trs) == 1:
-                t = trs[0]
-                return g.remote_dma(t[1], t[0], T.sem[t[3]], T.sem["sent"], dst[1], dst[0], sum(1 << e for e in t[2]))
-            return g.remote_dma_fused([RemoteDMATransfer(dst_ids=[DstId(rid=dst[0], pnc=dst[1])],
-                                                         dma_engine_mask=sum(1 << e for e in t[2]),
-                                                         remote_sem=T.sem[t[3]], src=t[0], dst=t[1]) for t in trs],
-                                      local_sem=T.sem["sent"])
-        s = add("G", go, rd, [], "send", 0, cnt=sum(len(t[2]) for t in trs))
-        for name in sorted(set(t[3] for t in trs)):
-            mine = [t for t in trs if t[3] == name]
-            add(None, None, [], [r for t in mine for r in t[4]], "recv", sum(128 * t[5] for t in trs), extra=[s],
-                sem=name, cnt=sum(len(t[2]) for t in mine))
+    def send(src, to, sem, rd, land, nbytes):
+        s = add("G", lambda: g.remote_dma(to, src, T.sem[sem], T.sem["sent"], dst[1], dst[0], mask), rd, [], "send", 0,
+                cnt=len(engines))
+        add(None, None, [], [land], "recv", 128 * nbytes, extra=[s], sem=sem, cnt=len(engines))
 
     def al(n):
         return (n, 0, 1 << 20)
@@ -148,11 +151,11 @@ def build(g, T, dst, engines, cfg):
             return add("G", lambda: g.iota(out, pat, base, cm, allow_small_or_imprecise_dtypes=True), [], wr, "g", n)
         return add("G", lambda: g.iota(out, pat, base, cm), [], wr, "g", n)
 
-    dma("Y", T["sli"][:], T.slot[:], [], [al("sli")], 8192)
-    dma("S", T["tri"][:], T.trav[:], [], [al("tri")], 131072)
-    dma("Y", T["X"][:], T.clk[:], [], [al("X")], 1048576)
-    dma("S", T["tti"][:], T.ttab[:], [], [al("tti")], 1572864)
-    dma("Y", T["lst"][:], T.last[:], [], [al("lst")], 1638400)
+    dma("Y", T["tri"][:], T.trav[:], [], [al("tri")], 131072)
+    dma("S", T["sli"][:], T.slot[:], [], [al("sli")], 8192)
+    dma("Y", T["X0"][:, 0:W], T.clk[:], [], [("X0", 0, W)], 1179648)
+    dma("Y", T["tti"][:], T.ttab[:], [], [al("tti")], 1703936)
+    dma("Y", T["ci"][:, 0:L], T.last[:], [], [("ci", 0, L)], 1769472)
 
     pI, col, J = T["pI"], T["col"], T["J"]
     iota(pI[:, 0:1], [[1, 1]], 0, 1, [("pI", 0, 1)], 1, False)
@@ -179,221 +182,248 @@ def build(g, T, dst, engines, cfg):
     ts(pc(3), pc(0), 4, 1, A.arith_shift_right, A.bitwise_and, [rp(0)], [rp(3)], 1)
     ts(pc(4), pc(0), 7, None, A.bitwise_and, None, [rp(0)], [rp(4)], 1)
     cp(col[:, 0:5], pI[:, 0:5], [("pI", 0, 5)], [("col", 0, 5)], 5)
-    ts(cc(5), cc(0), 16.0, None, A.add, None, [rc(0)], [rc(5)], 1)
+    ts(cc(13), cc(0), 16.0, None, A.add, None, [rc(0)], [rc(13)], 1)
     ts(cc(6), cc(2), 16.0, 15.0, A.mult, A.add, [rc(2)], [rc(6)], 1)
     ts(cc(7), cc(3), -1.0, 1.0, A.mult, A.add, [rc(3)], [rc(7)], 1)
-    ts(cc(8), cc(4), -1024.0, 15360.0, A.mult, A.add, [rc(4)], [rc(8)], 1)
+    ts(cc(8), cc(4), -1024.0, 207.0 * 1024, A.mult, A.add, [rc(4)], [rc(8)], 1)
     ts(cc(9), cc(1), 2452.0, -0.25, A.mult, A.add, [rc(1)], [rc(9)], 1)
-    ts(cc(10), cc(1), 16.0 - 4 * cfg["NSQ"], -8.0, A.is_ge, A.mult, [rc(1)], [rc(10)], 1)
-    ts(cc(11), cc(10), 20.0 if cfg["RS"] else 28.0, None, A.add, None, [rc(10)], [rc(11)], 1)
     ts(cc(12), cc(0), -1.0, 127.0, A.mult, A.add, [rc(0)], [rc(12)], 1)
-    for name, f in (("I", 1.0), ("nId", -1.0), ("I16", 8.0 if cfg["RS"] else 16.0), ("IK", 3.0 * 2 ** 24), ("Ih", 0.5)):
+    need = {}
+    for a, b in pieces(cfg["P3"]):
+        nc, nq = classes(b - a), cfg["NSQ"][a]
+        if (nc, nq) not in need:
+            k = need[nc, nq] = 14 + len(need)
+            ts(pc(5), pc(0), nc - 1, None, A.bitwise_and, None, [rp(0)], [rp(5)], 1)
+            ts(cc(10), pc(5), float(nc - nq), -8.0, A.is_ge, A.mult, [rp(5)], [rc(10)], 1)
+            ts(cc(k), cc(10), 28.0, None, A.add, None, [rc(10)], [rc(k)], 1)
+    for name, f in (("I", 1.0), ("nI_", -1.0), ("Ih", 0.5), ("I16", 16.0), ("NH", -1024.0),
+                    ("NK", -2.0 ** 26), ("If", 1.0), ("nIf", -1.0)):
         ts(T[name][:], J[:, 0:128], cc(0), f, A.is_equal, A.mult, [al("J"), rc(0)], [al(name)], 128)
     ts(T["CKa"][:], J[:, 0:128], cc(0), cc(8), A.is_equal, A.mult, [al("J"), rc(0), rc(8)], [al("CKa")], 128)
-    ts(T["CKb"][:], J[:, 0:128], cc(12), -2.0 ** 26, A.is_equal, A.mult, [al("J"), rc(12)], [al("CKb")], 128)
+    ts(T["CKb"][:], J[:, 0:128], cc(12), -2.0 ** 24, A.is_equal, A.mult, [al("J"), rc(12)], [al("CKb")], 128)
     tt(T["CK"][:], T["CKa"][:], T["CKb"][:], A.add, [al("CKa"), al("CKb")], [al("CK")], 128, 2)
-    ts(T["BO"][:], T["Jg"][:], cc(2), 0.5, A.is_equal, A.mult, [al("Jg"), rc(2)], [al("BO")], 128)
+    ts(T["BO"][:], T["Jg"][:], cc(2), None, A.is_equal, None, [al("Jg"), rc(2)], [al("BO")], 128)
     for name, f in (("W1", 1.0), ("W8", 8192.0), ("Wh", 0.5)):
         ts(T[name][:], J[:, 0:144], cc(6), f, A.is_equal, A.mult, [al("J"), rc(6)], [al(name)], 144)
-    ts(T["WI0"][:], J[:], cc(5), cc(7), A.is_equal, A.mult, [al("J"), rc(5), rc(7)], [al("WI0")], 160)
-    ts(T["WI1"][:], J[:], cc(5), cc(3), A.is_equal, A.mult, [al("J"), rc(5), rc(3)], [al("WI1")], 160)
-    iota(T["SLT"][:], [[0, 16], [0, 144]], 0, 0, [al("SLT")], 2304)
+    ts(T["WI0"][:], J[:], cc(13), cc(7), A.is_equal, A.mult, [al("J"), rc(13), rc(7)], [al("WI0")], 160)
+    ts(T["WI1"][:], J[:], cc(13), cc(3), A.is_equal, A.mult, [al("J"), rc(13), rc(3)], [al("WI1")], 160)
+    for r in range(0, 16, 4):
+        iota(T["SLT"][:, r:r + 4, :], [[0, 4], [0, 144]], 0, 0, [("SLT", r, r + 4)], 576)
     ts(T["t1"][:], T["Jr"][:], cc(1), 8192.0, A.is_gt, A.mult, [al("Jr"), rc(1)], [al("t1")], 128)
     ts(T["t2"][:], T["Jh"][:], cc(2), None, A.is_equal, None, [al("Jh"), rc(2)], [al("t2")], 128)
     tt(T["SLT"][:, :, 15:143:16], T["t1"][:], T["t2"][:], A.mult, [al("t1"), al("t2")], [al("SLT")], 128, 2)
-    nsc = 16 * max(b - a for a, b in pieces(cfg["P2"]))
-    iota(T["rmin"][:, 0:nsc], [[0, nsc // 16], [-256, 16]], 255, 0, [al("rmin")], nsc)
-    iota(T["rmax"][:, 0:nsc], [[0, nsc // 16], [256, 16]], 0, 0, [al("rmax")], nsc)
+    nsc = 16 * max(b - a for a, b in pieces(cfg["PM"]))
+    for s in range(0, 16 * max(b - a for a, b in pieces(cfg["P2"])), 512):
+        iota(T["rmin"][:, s:s + 512], [[0, 32], [-256, 16]], 255, 0, [("rmin", s, s + 512)], 512)
+    ms(T["rmax"][:, 0:nsc], 256.0, [al("rmax")], nsc)
+    ms(T["rmax"][:, 0:nsc:16], 0.0, [al("rmax")], nsc // 16)
     ms(T["rk"][:], 0.0, [al("rk")], L)
     ms(T["rk"][:, 0:L:8], -2.0 ** 28, [al("rk")], 32)
     ms(T["ones"][:], 1.0, [al("ones")], 128)
-    if cfg["S8"]:
-        ms(T["neg"][:], -1.0, [al("neg")], L)
     iota(T["CLi"][:, 0:16], [[1, 16]], 0, 0, [("CLi", 0, 16)], 16, False)
     iota(T["CLi"][:, 16:32], [[2, 8], [0, 2]], 0, 0, [("CLi", 16, 32)], 16, False)
-    cp(T["CL"][:], T["CLi"][:], [al("CLi")], [al("CL")], 32)
-    ms(T["bnd"][:, 0:1], 0.0, [("bnd", 0, 1)], 1)
-    add("S", lambda: S.activation(T["C4"][:], T["IOT"][:], F.Identity, bias=cc(9), scale=148.0), [al("IOT"), rc(9)],
-        [al("C4")], "s", B)
+    gc_(T["CL"][:], T["CLi"][:], [al("CLi")], [al("CL")], 32)
+    ms(T["bnd"][:, 0:1], 256.0, [("bnd", 0, 1)], 1)
+    act(T["C4"][:], T["IOT"][:], F.Identity, [al("IOT"), rc(9)], [al("C4")], B, bias=cc(9), scale=148.0)
     ts(T["LD"][:], T["J16"][:], cc(1), float(B), A.add, A.add, [al("J16"), rc(1)], [al("LD")], 16)
     ts(T["L16"][:], T["J16"][:], cc(1), 16.0, A.add, A.mult, [al("J16"), rc(1)], [al("L16")], 16)
     cp(T["bu"][:, 0:16], T["sli"][:], [al("sli")], [("bu", 0, 16)], 16)
     cp(T["Tu"][:, 0:L], T["tri"][:], [al("tri")], [("Tu", 0, L)], L)
-    cp(T["Tf"][:, 0:L], T["tri"][:], [al("tri")], [("Tf", 0, L)], L)
-    cp(T["tt"][:, 0:B], T["tti"][:], [al("tti")], [("tt", 0, B)], B)
-    ts(T["ci"][:, 0:L], T["lst"][:], 1.0, None, A.add, None, [al("lst")], [("ci", 0, L)], L, 0.5)
+    for s in range(0, B, 256):
+        gc_(T["tt"][:, s:s + 256], T["tti"][:, s:s + 256], [al("tti")], [("tt", s, s + 256)], 256)
 
     def sel(name, k):
         return T[name][:, 15 - k:143 - k]
 
-    def lowest(lu, rlu, src, rsrc, out, rout):
-        E, b7 = T["E"], T["b7"]
-        act(T["brow"][:], T["IOT"][:, 0:B].indirect(lu), F.Copy, None, [al("IOT"), rlu], [al("brow")], L, "sg")
-        for k in range(2):
-            gtt(E[:, k * L:(k + 1) * L], src.indirect(T["CL"][:, 16 * k:16 * k + 16]), T["brow"][:], A.is_equal,
-                [rsrc, al("CL"), al("brow")], [("E", k, k + 1)], L)
-        mm([(b7[:, L:L + 16], T["SLT"][:, r, 15 - r:143 - r], E[:, r:L:16], r == 0, False, 16) for r in range(16)]
-           + [(b7[:, L + 1:L + 16:2], sel("W8", r), E[:, L + 16 + r:2 * L:32], False, r == 15, 8) for r in range(16)],
-           [al("E"), al("SLT"), al("W8")], [("b7", L, L + 16)])
-        tt(T["o1"][:], b7[:, L:L + 16], T["LD"][:], A.min, [("b7", L, L + 16), al("LD")], [al("o1")], 16)
-        tt(T["o2"][:], T["o1"][:], src, A.max, [al("o1"), rsrc], [al("o2")], 16)
-        cvt("o", out, T["o2"][:], [al("o2")], [rout], 16)
+    def reg(r, a, b):
+        bank, s = "a%d" % (a // BK), BK * r + a % BK
+        return T[bank][:, s:s + b - a], (bank, s, s + b - a), al("g" + bank)
 
-    lowest(T["bu"][:, 0:16], ("bu", 0, 16), T["sli"][:], al("sli"), T["off"][:, 0:16], ("off", 0, 16))
-
-    X, tab, vp, b0, b7, kp = T["X"], T["tt"], T["vp"], T["b0"], T["b7"], T["kp"]
-    e, ap, mn, mx = T["e"], T["b7"], T["mn"], T["mx"]
+    tab, kp, sm = T["tt"], T["kp"], T["ms"]
+    e, mn, mx = T["e"], T["mn"], T["mx"]
+    I, If, nIf, ones = T["I"][:], T["If"][:], T["nIf"][:], T["ones"]
     dturn = [0]
 
+    def dbank():
+        dturn[0] += 1
+        return DB[dturn[0] % len(DB)]
+
     def cut(a, b):
-        return [(s, min(b, s + cfg["G"])) for s in range(a, b, cfg["G"])]
+        return [(s, min(b, s + cfg["G"])) for s in range(a, b, cfg["G"])][::-1]
     for v in range(NV):
         visit[0] = v
         last = v == NV - 1
         o, ob = v * L, v * 16
-        if last:
-            dma("Y", T["X2"][:], X[:], [al("X")], [al("X2")], 1048576)
+        xn, xo = "X%d" % (v % 2), "X%d" % (1 - v % 2)
+        X = T[xn]
+        dma("Y", T[xo][:, 0:W], X[:, 0:W], [(xn, 0, W), ("bu", ob, ob + 16), ("ci", o, o + L)], [(xo, 0, W)], 1048576)
         for a, b in pieces(cfg["PX"]):
-            act(T["x"][:, 16 * a:16 * b], X[:, 0:W].indirect(T["Tu"][:, o + a:o + b]), F.Copy, None,
-                [al("X"), ("Tu", o + a, o + b)], [("x", a, b)], 16 * (b - a), "sg")
+            win, rd = X[:, 0:W].indirect(T["Tu"][:, o + a:o + b]), [al(xn), ("Tu", o + a, o + b)]
+            if a in cfg["XV"]:
+                gcp(T["x"][:, 16 * a:16 * b], win, rd, [("x", a, b)], 16 * (b - a))
+            else:
+                act(T["x"][:, 16 * a:16 * b], win, F.Copy, rd, [("x", a, b)], 16 * (b - a), "sg")
+        for a, b in pieces([0, 128, 256]):
+            gc_(T["Tf"][:, a:b], T["Tu"][:, o + a:o + b], [("Tu", o + a, o + b)], [("Tf", a, b)], b - a)
+            bl, rbl = T["bu"][:, ob + a // 16:ob + b // 16], ("bu", ob + a // 16, ob + b // 16)
+            act(T["brC"][:, a:b], T["C4"][:, 0:B].indirect(bl), F.Copy, [al("C4"), rbl], [("brC", a, b)], b - a, "sg")
         for a, b in pieces(cfg["P1"]):
             n = b - a
             bl, rbl = T["bu"][:, ob + a // 16:ob + b // 16], ("bu", ob + a // 16, ob + b // 16)
-            Tf, rT = T["Tf"][:, o + a:o + b], ("Tf", o + a, o + b)
             tn = "tt" if v else "tti"
-            gcp(T["Hu"][:, a:b], T[tn][:, 0:B].indirect(bl), [al(tn), rbl], [("Hu", a, b)], n)
-            gtt(T["D"][:, a:b], T[tn][:, 0:B].indirect(bl), Tf, A.subtract, [al(tn), rbl, rT], [("D", a, b)], n)
+            (p0, r0, gr), (p1, r1, _), (p2, r2, _) = reg(0, a, b), reg(1, a, b), reg(2, a, b)
+            if b in cfg["PH"]:
+                ah = cfg["PH"][cfg["PH"].index(b) - 1]
+                gcp(T["Hu"][:, ah:b], T[tn][:, 0:B].indirect(T["bu"][:, ob + ah // 16:ob + b // 16]),
+                    [al(tn), ("bu", ob + ah // 16, ob + b // 16)], [("Hu", ah, b)], b - ah)
+                gc_(T["Hf"][:, ah:b], T["Hu"][:, ah:b], [("Hu", ah, b)], [("Hf", ah, b)], b - ah)
+            mm([(p1, If, T["Hf"][:, a:b], n, 4), (p1, nIf, T["Tf"][:, a:b], n, 4)],
+               [("Hf", a, b), ("Tf", a, b), al("If"), al("nIf"), gr], [r1])
             for a2, b2 in cut(a, b):
                 gtt(T["c1"][:, 16 * a2:16 * b2], X[:, 0:W].indirect(T["Hu"][:, a2:b2]), T["x"][:, 16 * a2:16 * b2], A.is_ge,
-                    [al("X"), ("Hu", a2, b2), ("x", a2, b2)], [("c1", a2, b2)], 16 * (b2 - a2))
-            mm([(b0[:, a:b], sel("W1", k), T["c1"][:, 16 * a + k:16 * b:16], k == 0, k == 15, n) for k in range(16)],
-               [("c1", a, b), al("W1")], [("b0", a, b)])
-            ts(vp[:, a:b], b0[:, a:b], T["bnd"][:, v:v + 1], 9.0, A.subtract, A.is_ge, [("b0", a, b), ("bnd", v, v + 1)],
-               [("vp", a, b)], n)
-            tt(vp[:, a:b], vp[:, a:b], T["D"][:, a:b], A.mult, [("vp", a, b), ("D", a, b)], [("vp", a, b)], n)
-            tt(T["T1"][:, a:b], vp[:, a:b], Tf, A.add, [("vp", a, b), rT], [("T1", a, b)], n)
-            cp(T["T1u"][:, a:b], T["T1"][:, a:b], [("T1", a, b)], [("T1u", a, b)], n)
+                    [al(xn), ("Hu", a2, b2), ("x", a2, b2)], [("c1", a2, b2)], 16 * (b2 - a2))
+            p0, r0, gr0 = reg(3, a ^ 128, (a ^ 128) + n) if BK == 128 else reg(0, a, b)
+            mm([(p0, sel("W1", k), T["c1"][:, 16 * a + k:16 * b:16], n, 1) for k in range(16)], [("c1", a, b), al("W1"), gr0], [r0])
+            ts(T["tk"][:, a:b], p0, T["bnd"][:, v:v + 1], 265.0, A.add, A.is_ge, [r0, ("bnd", v, v + 1)], [("tk", a, b)], n)
+            tt(T["u"][:, a:b], p1, T["tk"][:, a:b], A.mult, [r1, ("tk", a, b)], [("u", a, b)], n)
+            mm([(p2, If, T["Tf"][:, a:b], n, 4), (p2, If, T["u"][:, a:b], n, 4)], [("u", a, b), ("Tf", a, b), al("If"), gr], [r2])
+            cp(T["T1u"][:, a:b], p2, [r2], [("T1u", a, b)], n)
+            gc_(T["T1"][:, a:b], T["T1u"][:, a:b], [("T1u", a, b)], [("T1", a, b)], n)
             for a2, b2 in cut(a, b):
-                act(T["z"][:, 16 * a2:16 * b2], X[:, 0:W].indirect(T["T1u"][:, a2:b2]), F.Copy, None,
-                    [al("X"), ("T1u", a2, b2)], [("z", a2, b2)], 16 * (b2 - a2), "sg")
+                act(T["z"][:, 16 * a2:16 * b2], X[:, 0:W].indirect(T["T1u"][:, a2:b2]), F.Copy,
+                    [al(xn), ("T1u", a2, b2)], [("z", a2, b2)], 16 * (b2 - a2), "sg")
         for a, b in pieces(cfg["P2"]):
             n = b - a
             zz = T["z"][:, 16 * a:16 * b]
             vop(lambda a=a, b=b, n=n, zz=zz: V.tensor_tensor_scan(mn[:, 16 * a:16 * b], T["rmin"][:, 0:16 * n], zz, 0.0, A.max, A.min),
                 [("z", a, b), al("rmin")], [("mn", a, b)], 16 * n, 0.5)
-            vop(lambda a=a, b=b, n=n, zz=zz: V.tensor_tensor_scan(mx[:, 16 * a:16 * b], T["rmax"][:, 0:16 * n], zz, 0.0, A.min, A.max),
-                [("z", a, b), al("rmax")], [("mx", a, b)], 16 * n, 0.5)
-            m = mn[:, 16 * a + 15:16 * b:16]
-            ra = ("b7", a, b)
-            mm([(ap[:, a:b], T["I"][:], m, True, False, n), (ap[:, a:b], T["Ih"][:], T["ones"][:, 0:n], False, True, n)],
-               [("mn", a, b), al("I"), al("Ih"), al("ones")], [ra])
-            act(T["co"][:, o + a:o + b], m, F.Identity, 0.0 if last else 1.0, [("mn", a, b)], [("co", o + a, o + b)], n)
-            tt(T["prod"][:, a:b], ap[:, a:b], T["T1"][:, a:b], A.mult, [ra, ("T1", a, b)], [("prod", a, b)], n)
-            gtt(T["qI"][:, a:b], T["C4"][:, 0:B].indirect(T["bu"][:, ob + a // 16:ob + b // 16]), T["prod"][:, a:b], A.add,
-                [al("C4"), ("bu", ob + a // 16, ob + b // 16), ("prod", a, b)], [("qI", a, b)], n)
+            if a in cfg["PM"]:
+                bm = cfg["PM"][cfg["PM"].index(a) + 1]
+                vop(lambda a=a, b=bm: V.tensor_tensor_scan(mx[:, 16 * a:16 * b], T["rmax"][:, 0:16 * (b - a)], T["z"][:, 16 * a:16 * b],
+                                                           0.0, A.min, A.max), [("z", a, bm), al("rmax")], [("mx", a, bm)], 16 * (bm - a), 0.5)
+            m, rm = mn[:, 16 * a + 15:16 * b:16], ("mn", a, b)
+            (p0, r0, gr), (p1, r1, _), (p2, r2, _) = reg(0, a, b), reg(1, a, b), reg(2, a, b)
+            mm([(p0, I, m, n, 1), (p0, T["Ih"][:], ones[:, 0:n], n, 1)], [rm, al("I"), al("Ih"), al("ones"), gr], [r0])
+            tt(p1, p0, T["T1"][:, a:b], A.mult, [r0, ("T1", a, b)], [r1], n)
+            tt(T["qI"][:, a:b], p1, T["brC"][:, a:b], A.add, [r1, ("brC", a, b)], [("qI", a, b)], n)
             ts(T["nI"][:, a:b], T["qI"][:, a:b], 2, W - 1, A.arith_shift_right, A.bitwise_and, [("qI", a, b)], [("nI", a, b)], n)
             cp(T["nu"][:, a:b], T["nI"][:, a:b], [("nI", a, b)], [("nu", a, b)], n)
-            if cfg["RS"]:
-                dn = "d%d" % (dturn[0] % 4)
-                dturn[0] += 1
-                mm([(T[dn][:, 0:n], T["I"][:], m, True, False, n),
-                    (T[dn][:, 0:n], T["nId"][:], T["ci"][:, o + a:o + b], False, True, n)],
-                   [("mn", a, b), ("ci", o + a, o + b), al("I"), al("nId")], [al(dn)])
-                act(T["rel"][:, a:b], T[dn][:, 0:n], F.Sign, 0.5, [al(dn)], [("rel", a, b)], n)
-            else:
-                tt(T["rel"][:, a:b], ap[:, a:b], T["ci"][:, o + a:o + b], A.is_gt, [ra, ("ci", o + a, o + b)],
-                   [("rel", a, b)], n)
-            ts(T["n10"][:, a:b], T["qI"][:, a:b], 2, B - 1, A.arith_shift_right, A.bitwise_and, [("qI", a, b)], [("n10", a, b)], n)
-            tt(vp[:, L + a:L + b], T["nI"][:, a:b], T["T1"][:, a:b], A.subtract, [("nI", a, b), ("T1", a, b)],
-               [("vp", L + a, L + b)], n, 2)
+            gc_(T["nf"][:, a:b], T["nI"][:, a:b], [("nI", a, b)], [("nf", a, b)], n)
+            if a in cfg["PC"]:
+                bm = cfg["PC"][cfg["PC"].index(a) + 1]
+                gc_(T["co"][:, o + a:o + bm], mn[:, 16 * a + 15:16 * bm:16], [("mn", a, bm)], [("co", o + a, o + bm)], bm - a)
+                hb = 192.0 - 511.5 / 1024
+                if cfg["HS"]:
+                    act(T["hh"][:, a:bm], T["nf"][:, a:bm], F.Identity, [("nf", a, bm)], [("hh", a, bm)], bm - a, bias=hb, scale=1.0 / 1024)
+                else:
+                    ts(T["hh"][:, a:bm], T["nu"][:, a:bm], 1.0 / 1024, hb, A.mult, A.add, [("nu", a, bm)], [("hh", a, bm)], bm - a, 0.5)
+            mm([(p2, If, T["T1"][:, a:b], n, 4), (p2, nIf, T["nf"][:, a:b], n, 4)],
+               [("T1", a, b), ("nf", a, b), al("If"), al("nIf"), gr], [r2])
         if last:
             dma("Y", T.ylast[:], T["co"][:, o:o + L], [("co", o, o + L)], [], 65536)
-        mm([(b7[:, 272:288], sel("W1", r), mx[:, 16 * r + 15:W:256], r == 0, r == 15, 16) for r in range(16)],
-           [al("mx"), al("W1")], [("b7", 272, 288)])
-        cp(T["uI"][:], b7[:, 272:288], [("b7", 272, 288)], [al("uI")], 16)
+        else:
+            send(T["co"][:, o:o + L], T["ci"][:, o + L:o + 2 * L], "c%d_0" % (v + 1), [("co", o, o + L)],
+                 ("ci", o + L, o + 2 * L), 2 * L)
+        mm([(sm[:, 0:16], sel("W1", r), mx[:, 16 * r + 15:W:256], 16, 1) for r in range(16)], [al("mx"), al("W1")], [("ms", 0, 16)])
+        cp(T["uI"][:], sm[:, 0:16], [("ms", 0, 16)], [al("uI")], 16)
         ts(T["uA"][:], T["uI"][:], 15, None, A.bitwise_and, None, [al("uI")], [al("uA")], 16)
         tt(T["jI"][:], T["uA"][:], T["L16"][:], A.add, [al("uA"), al("L16")], [al("jI")], 16)
-        cvt("j", T["ju"][:], T["jI"][:], [al("jI")], [al("ju")], 16)
+        gc_(T["ju"][:], T["jI"][:], [al("jI")], [al("ju")], 16)
         if cfg["S8"]:
-            s8 = T["s8b"]
-            act(T["xj"][:], X[:, 0:W].indirect(T["ju"][:]), F.Copy, None, [al("X"), al("ju")], [al("xj")], L, "sg")
-            mm([(b0[:, 0:L], T["I"][:], T["xj"][:], True, False, L), (b0[:, 0:L], T["I"][:], mx[:, 15:W:16], False, False, L),
-                (b0[:, 0:L], T["Ih"][:], T["neg"][:], False, True, L)], [al("xj"), al("mx"), al("I"), al("Ih"), al("neg")],
-               [("b0", 0, L)])
-            add("S", lambda: S.activation(T["s8"][:], b0[:, 0:L], F.Identity, bias=1.5 * 2 ** 23, scale=0.5), [("b0", 0, L)],
-                [al("s8")], "s", L)
-            act(s8[:], T["s8"][:], F.Identity, -1.5 * 2 ** 23, [al("s8")], [al("s8i")], L)
+            act(T["s8"][:], X[:, 0:W].indirect(T["ju"][:]), F.Identity, [al(xn), al("ju")], [al("s8")], L, "sg", bias=-0.25, scale=0.5)
+            mm([(sm[:, L:2 * L], T["Ih"][:], mx[:, 15:W:16], L, 1)], [al("mx"), al("Ih")], [("ms", L, 2 * L)])
+            tt(T["s8i"][:], sm[:, L:2 * L], T["s8"][:], A.add, [("ms", L, 2 * L), al("s8")], [al("s8i")], L)
         else:
-            s8 = T["s8i"]
-            gtt(T["s8"][:], X[:, 0:W].indirect(T["ju"][:]), mx[:, 15:W:16], A.add, [al("X"), al("ju"), al("mx")], [al("s8")], L)
-            ts(s8[:], T["s8"][:], 0.5, -0.25, A.mult, A.add, [al("s8")], [al("s8i")], L)
+            gtt(T["s8"][:], X[:, 0:W].indirect(T["ju"][:]), mx[:, 15:W:16], A.add, [al(xn), al("ju"), al("mx")], [al("s8")], L)
+            ts(T["s8i"][:], T["s8"][:], 0.5, -0.25, A.mult, A.add, [al("s8")], [al("s8i")], L)
+        gcp(T[xo][:, 0:W].indirect(T["ju"][:]), T["s8i"][:], [al("s8i"), al("ju")], [(xo, 0, W)], L, "vs")
         if last:
-            gcp(T["X2"][:, 0:W].indirect(T["ju"][:]), s8[:], [al("s8i"), al("ju")], [al("X2")], L, "vs")
-            dma("Y", T.yclk[:], T["X2"][:], [al("X2")], [], 1048576)
-        ts(T["FB"][:], T["bu"][:, ob:ob + 16], 97.0 - 2 ** 24, None, A.add, None, [("bu", ob, ob + 16)], [al("FB")], 16)
-        for ch, (a, b) in enumerate(pieces(cfg["P3"])):
-            n = b - a
+            dma("Y", T.yclk[:], T[xo][:, 0:W], [(xo, 0, W)], [], 1048576)
+        bl, rbl = T["bu"][:, ob:ob + 16], ("bu", ob, ob + 16)
+        gc_(T["bfl"][:], bl, [rbl], [al("bfl")], 16)
+        if cfg["FS"]:
+            act(T["FB"][:], T["bfl"][:], F.Identity, [al("bfl")], [al("FB")], 16, bias=97.0 - 2 ** 24)
+            act(T["sC"][:], T["bfl"][:], F.Identity, [al("bfl"), rc(9)], [al("sC")], 16, bias=cc(9), scale=148.0)
+        else:
+            ts(T["FB"][:], bl, 97.0 - 2 ** 24, None, A.add, None, [rbl], [al("FB")], 16)
+            ts(T["sC"][:], bl, 148.0, cc(9), A.mult, A.add, [rbl, rc(9)], [al("sC")], 16)
+        E = T["E"]
+        for k in range(2):
+            gtt(E[:, k * L:(k + 1) * L], T["sC"][:, 0:16].indirect(T["CL"][:, 16 * k:16 * k + 16]), T["brC"][:], A.is_equal,
+                [al("sC"), al("CL"), al("brC")], [("E", k, k + 1)], L)
+        lst = ([(sm[:, 16:32], If, T["bfl"][:], 16, 4)]
+               + [(sm[:, 16:32], T["SLT"][:, r, 15 - r:143 - r], E[:, r:L:16], 16, 1) for r in range(16)]
+               + [(sm[:, 17:32:2], sel("W8", r), E[:, L + 16 + r:2 * L:32], 8, 1) for r in range(16)])
+        mm(lst, [al("E"), al("SLT"), al("W8"), al("bfl"), al("If")], [("ms", 16, 32)])
+        tt(T["o1"][:], sm[:, 16:32], T["LD"][:], A.min, [("ms", 16, 32), al("LD")], [al("o1")], 16)
+        gc_(T["off"][:], T["o1"][:], [al("o1")], [al("off")], 16)
+        for a, b in pieces(cfg["P3"]):
+            n, nsq = b - a, cfg["NSQ"][a]
+            nc = classes(n)
+            nr = 16 // nc
             for a2, b2 in cut(a, b):
-                act(e[:, 16 * a2:16 * b2], X[:, 0:W].indirect(T["nu"][:, a2:b2]), F.Identity, 1.0, [al("X"), ("nu", a2, b2)],
+                act(e[:, 16 * a2:16 * b2], X[:, 0:W].indirect(T["nu"][:, a2:b2]), F.Copy, [al(xn), ("nu", a2, b2)],
                     [("e", a2, b2)], 16 * (b2 - a2), "sg")
             M, m = mx[:, 16 * a + 15:16 * b:16], mn[:, 16 * a + 15:16 * b:16]
 
-            def diff(q, y, ry, fn, bias, out):
-                dn = "d%d" % (dturn[0] % 4)
-                dturn[0] += 1
-                lst = []
-                for r in range(4):
-                    lst += [(T[dn][:, r * n:(r + 1) * n], T["I"][:], e[:, 16 * a + 4 * q + r:16 * b:16], True, False, n),
-                            (T[dn][:, r * n:(r + 1) * n], T["nId"][:], y, False, True, n)]
-                mm(lst, [("e", a, b), ry, al("I"), al("nId")], [al(dn)])
-                s0 = 16 * a + 4 * q * n
-                act(T[out][:, s0:s0 + 4 * n], T[dn][:, 0:4 * n], fn, bias, [al(dn)], [(out, s0, s0 + 4 * n)], 4 * n)
-            lst = []
-            for q in range(4):
-                onv = q < 4 - cfg["NSQ"]
-                if not onv:
-                    diff(q, m, ("mn", a, b), F.Sign, -0.5, "sg")
-                for p in range(4 * q, 4 * q + 4):
-                    s0 = 16 * a + p * n
-                    if onv:
-                        tt(T["sg"][:, s0:s0 + n], e[:, 16 * a + p:16 * b:16], ap[:, a:b], A.is_gt,
-                           [("e", a, b), ("b7", a, b)], [("sg", s0, s0 + n)], n)
-                    lst.append((b0[:, L + a:L + b], sel("W1" if onv else "Wh", p), T["sg"][:, s0:s0 + n], p == 0, False, n))
-            lst.append((b0[:, L + a:L + b], T["I16"][:], T["rel"][:, a:b], False, True, n))
-            mm(lst, [("sg", 16 * a, 16 * b), ("rel", a, b), al("W1"), al("Wh"), al("I16")], [("b0", L + a, L + b)])
-            ts(T["rdy"][:, a:b], b0[:, L + a:L + b], cc(11), None, A.is_ge, None, [("b0", L + a, L + b), rc(11)], [("rdy", a, b)], n)
-            rv = ("vp", L + a, L + b)
-            tt(vp[:, L + a:L + b], vp[:, L + a:L + b], T["rdy"][:, a:b], A.mult, [rv, ("rdy", a, b)], [rv], n)
-            r2 = ("T2", o + a, o + b)
-            tt(T["T2"][:, o + a:o + b], vp[:, L + a:L + b], T["T1"][:, a:b], A.add, [rv, ("T1", a, b)], [r2], n)
-            if not last:
-                cvt("t", T["T2u"][:, o + a:o + b], T["T2"][:, o + a:o + b], [r2], [("T2u", o + a, o + b)], n)
-                h, d = (a + b) // 2, o + L
-                s0, s1 = "ar%d_%d_0" % (v + 1, ch), "ar%d_%d_1" % (v + 1, ch)
-                k = len(engines) // 4
-                es = [engines[i::4][:k] for i in range(4)]
-                send([(T["T2u"][:, o + a:o + b], T["Tu"][:, d + a:d + b], es[0], s0, [("Tu", d + a, d + b)], 2 * n),
-                      (T["T2"][:, o + a:o + h], T["Tf"][:, d + a:d + h], es[2], s1, [("Tf", d + a, d + h)], 2 * n),
-                      (T["T2"][:, o + h:o + b], T["Tf"][:, d + h:d + b], es[3], s1, [("Tf", d + h, d + b)], 2 * n),
-                      (T["co"][:, o + a:o + b], T["ci"][:, d + a:d + b], es[1], s1, [("ci", d + a, d + b)], 2 * n)],
-                     [r2, ("T2u", o + a, o + b), ("co", o + a, o + b)])
+            def cls(t, q):
+                return t[:, 16 * a + q:16 * b:nc]
+
+            def diff(q, y, ry, fn, out, **kw):
+                dn = dbank()
+                mm([(T[dn][:, r:nr * n:nr], T["nI_"][:], y, n, 1) for r in range(nr)], [ry, al("nI_")], [al(dn), al("g" + dn)])
+                mm([(T[dn][:, 0:nr * n], I, cls(e, q), nr * n, 1)], [("e", a, b), al("I"), al("g" + dn)], [al(dn)], False)
+                act(cls(T[out], q), T[dn][:, 0:nr * n], fn, [al(dn)], [(out + str(q), a, b)], nr * n, **kw)
+            (p0, r0, gr), (p2, r2, _) = reg(0, a, b), reg(2, a, b)
+            todo = [("ab", q) for q in range(nc)]
+            todo[cfg["SGAT"][a]:cfg["SGAT"][a]] = [("sg", q) for q in range(nc - nsq, nc)]
+            for kind, q in todo:
+                if kind == "ab":
+                    diff(q, M, ("mx", a, b), F.Abs, "ab")
+                else:
+                    diff(q, m, ("mn", a, b), F.Sign, "sg", bias=0.5)
+            if BK == 128:
+                mr, m0, rmr, nv, gm = T["a2"], 0, al("a2"), nr, []
+            else:
+                mr, m0, rmr, nv, gm = T[r0[0]], 256, (r0[0], 256, 512), 4, [gr]
+            mm([(mr[:, m0 + r:m0 + nv * n:nv], I, m, n, 1) for r in range(nv)], [("mn", a, b), al("I")] + gm, [rmr])
+            tt(T["rel"][:, a:b], mr[:, m0:m0 + nv * n:nv], T["ci"][:, o + a:o + b], A.is_gt, [rmr, ("ci", o + a, o + b)],
+               [("rel", a, b)], n)
+            for q in range(nc - nsq):
+                for s in range(q, 16 // nv, nc):
+                    tt(T["sg"][:, 16 * a + s:16 * b:16 // nv], e[:, 16 * a + s:16 * b:16 // nv], mr[:, m0:m0 + nv * n], A.is_ge,
+                       [("e", a, b), rmr], [("sg%d" % q, a, b)] if s == q else [("sh%d" % q, a, b)], nv * n)
+            for q in range(nc):
+                onv = q < nc - nsq
+                mm([(p0, sel("W1" if onv else "Wh", p), T["sg"][:, 16 * a + p:16 * b:16], n, 1) for p in range(q, 16, nc)]
+                   + ([] if q else [(p0, T["I16"][:], T["rel"][:, a:b], n, 1)]),
+                   [("sg%d" % q, a, b), ("sh%d" % q, a, b), al("W1"), al("Wh"), al("I16"), ("rel", a, b)], [r0, gr], q == 0)
+            kb = need[nc, nsq]
+            ts(T["nr"][:, a:b], p0, cc(kb), None, A.is_lt, None, [r0, rc(kb)], [("nr", a, b)], n)
+            tt(p2, p2, T["nr"][:, a:b], A.mult, [r2, ("nr", a, b)], [r2], n)
+            tt(T["T2"][:, a:b], p2, T["nf"][:, a:b], A.add, [r2, ("nf", a, b)], [("T2", a, b)], n)
+            if not last and a in cfg["PT"]:
+                bt = cfg["PT"][cfg["PT"].index(a) + 1]
+                cvt("t", T["T2u"][:, o + a:o + bt], T["T2"][:, a:bt], [("T2", a, bt)], [("T2u", o + a, o + bt)], bt - a)
+                send(T["T2u"][:, o + a:o + bt], T["Tu"][:, o + L + a:o + L + bt], "t%d_%d" % (v + 1, a), [("T2u", o + a, o + bt)],
+                     ("Tu", o + L + a, o + L + bt), 2 * (bt - a))
             for a5 in range(b - 32, a - 1, -32):
-                gcp(tab[:, 0:B + L].indirect(T["off"][:, ob + a5 // 16:ob + a5 // 16 + 2]), T["T2"][:, o + a5:o + a5 + 32],
-                    [r2, ("off", ob, ob + 16)], [al("tt")], 32, "vs")
-            for q in range(4):
-                diff(q, M, ("mx", a, b), F.Abs, -1.0, "ab")
-                mm([(kp[:, a:b], sel("W8", p), T["ab"][:, 16 * a + p * n:16 * a + (p + 1) * n], p == 0, False, n)
-                    for p in range(4 * q, 4 * q + 4)],
-                   [("ab", 16 * a + 4 * q * n, 16 * a + 4 * (q + 1) * n), al("W8")], [("kp", a, b), al("kgrp")])
-            mm([(kp[:, a:b], T["CK"][:], T["ones"][:, 0:n], False, False, n), (kp[:, a:b], T["IK"][:], T["rdy"][:, a:b], False, True, n)],
-               [("rdy", a, b), al("CK"), al("IK"), al("ones")], [("kp", a, b), al("kgrp")])
+                gcp(tab[:, 0:B + L].indirect(T["off"][:, a5 // 16:a5 // 16 + 2]), T["T2"][:, a5:a5 + 32],
+                    [("T2", a, b), al("off")], [al("tt")], 32, "vs")
+            rk_ = [("kp", a, b), al("gk")]
+            mm([(kp[:, a:b], T["CK"][:], ones[:, 0:n], n, 1), (kp[:, a:b], T["NH"][:], T["hh"][:, a:b], n, 1),
+                (kp[:, a:b], If, T["nf"][:, a:b], n, 4)],
+               [("hh", a, b), ("nf", a, b), al("CK"), al("NH"), al("If"), al("ones")], rk_)
+            for q in range(nc):
+                mm([(kp[:, a:b], sel("W8", p), T["ab"][:, 16 * a + p:16 * b:16], n, 1) for p in range(q, 16, nc)],
+                   [("ab%d" % q, a, b), al("W8")] + rk_, [("k%d" % q, a, b)], False)
+            mm([(kp[:, a:b], T["NK"][:], T["nr"][:, a:b], n, 1)], [("nr", a, b), al("NK")] + rk_, [("k4", a, b)], False)
             if a not in cfg["P4"]:
                 continue
-            ch = cfg["P4"].index(a)
-            b = cfg["P4"][ch + 1]
+            b = cfg["P4"][cfg["P4"].index(a) + 1]
             n = b - a
-            tt(T["key"][:, a:b], kp[:, a:b], T["n10"][:, a:b], A.add, [("kp", a, b), ("n10", a, b)], [("key", a, b)], n)
-            vop(lambda a=a, b=b: V.transpose(T["kT"][:, a:b], T["key"][:, a:b]), [("key", a, b)], [("kT", a, b)], n)
+            vop(lambda a=a, b=b: V.transpose(T["kT"][:, a:b], kp[:, a:b]), [("kp", a, b)] + [("k%d" % q, a, b) for q in range(5)],
+                [("kT", a, b)], n)
             vop(lambda a=a, b=b, n=n: V.tensor_tensor_scan(T["ks"][:, a:b], T["rk"][:, 0:n], T["kT"][:, a:b], 0.0, A.add, A.max),
                 [("kT", a, b), al("rk")], [("ks", a, b)], n)
             a8, b8, a6, b6 = a // 8, b // 8, a // 16, b // 16
@@ -405,33 +435,30 @@ def build(g, T, dst, engines, cfg):
             for u in range(2):
                 for h in range(2):
                     s0 = 16 - 16 * (h - u)
-                    lst.append((b7[:, 288 + a6 + u:288 + b6:2], T["WI%d" % u][:, s0:s0 + 128], T["w"][:, a6 + h:b6:2],
-                                h == 0, h == 1, 8))
-            rw = ("b7", 288 + a6, 288 + b6)
-            mm(lst, [("w", a, b), al("WI0"), al("WI1")], [rw], 4)
-            tt(T["wI"][:, a6:b6], b7[:, 288 + a6:288 + b6], T["FB"][:, a6:b6], A.max, [rw, al("FB")], [("wI", a, b)], 16)
+                    lst.append((sm[:, 32 + a6 + u:32 + b6:2], T["WI%d" % u][:, s0:s0 + 128], T["w"][:, a6 + h:b6:2], 8, 4))
+            rw = ("ms", 32 + a6, 32 + b6)
+            mm(lst, [("w", a, b), al("WI0"), al("WI1")], [rw])
+            tt(T["wI"][:, a6:b6], sm[:, 32 + a6:32 + b6], T["FB"][:, a6:b6], A.max, [rw, al("FB")], [("wI", a, b)], 16)
             ts(T["bI"][:, a6:b6], T["wI"][:, a6:b6], B - 1, None, A.bitwise_and, None, [("wI", a, b)], [("bI", a, b)], 16)
             if last:
-                cp(T["ys"][:, a6:b6], T["bI"][:, a6:b6], [("bI", a, b)], [("ys", a, b)], 16)
+                gc_(T["ys"][:, a6:b6], T["bI"][:, a6:b6], [("bI", a, b)], [("ys", a, b)], b6 - a6)
             else:
                 rb = ("bo", ob + a6, ob + b6)
                 cvt("b", T["bo"][:, ob + a6:ob + b6], T["bI"][:, a6:b6], [("bI", a, b)], [rb], b6 - a6)
-                send([(T["bo"][:, ob + a6:ob + b6], T["bu"][:, ob + 16 + a6:ob + 16 + b6], engines, "ar%d_%d_2" % (v + 1, ch),
-                       [("bu", ob + 16 + a6, ob + 16 + b6)], n // 8)], [rb])
+                send(T["bo"][:, ob + a6:ob + b6], T["bu"][:, ob + 16 + a6:ob + 16 + b6], "b%d_%d" % (v + 1, a), [rb],
+                     ("bu", ob + 16 + a6, ob + 16 + b6), n // 8)
         if last:
             dma("Y", T.yttab[:], tab[:, 0:B], [al("tt")], [], 524288)
-            dma("Y", T.ytrav[:], T["T2"][:, o:o + L], [("T2", o, o + L)], [], 131072)
+            dma("Y", T.ytrav[:], T["T2"][:], [al("T2")], [], 131072)
             dma("Y", T.yslot[:], T["ys"][:], [al("ys")], [], 8192)
             break
-        gcp(X[:, 0:W].indirect(T["ju"][:]), s8[:], [al("s8i"), al("ju")], [al("X")], L, "vs")
-        mm([(b0[:, 0:L], T["BO"][:], T["rdy"][:], True, True, L)], [al("rdy"), al("BO")], [("b0", 0, L)])
-        add("S", lambda: S.activation(T["nh"][:], b0[:, 0:L], F.Sign, accum_out=T["r1"][:, 0:1]), [("b0", 0, L)],
-            [al("r1"), al("nh")], "s", L + 140)
-        ts(T["r2"][:, 0:1], T["r1"][:, 0:1], 1.5 * 2 ** 24, -1.5 * 2 ** 24, A.add, A.add, [al("r1")], [al("r2")], 1)
-        tt(T["bnd"][:, v + 1:v + 2], T["r1"][:, 0:1], T["r2"][:, 0:1], A.not_equal, [al("r1"), al("r2")], [("bnd", v + 1, v + 2)], 1)
-        lowest(T["bo"][:, ob:ob + 16], ("bo", ob, ob + 16), T["bI"][:], al("bI"), T["oo"][:, ob:ob + 16], ("oo", ob, ob + 16))
-        send([(T["oo"][:, ob:ob + 16], T["off"][:, ob + 16:ob + 32], engines, "of%d" % (v + 1), [("off", ob + 16, ob + 32)], 32)],
-             [("oo", ob, ob + 16)])
+        mm([(sm[:, 48:64], sel("W1", r), T["nr"][:, r:L:16], 16, 1) for r in range(16)], [al("nr"), al("W1")], [("ms", 48, 64)])
+        act(T["nh"][:], sm[:, 48:64], F.Sign, [("ms", 48, 64)], [al("r1"), al("nh")], 40, bias=16.0, scale=-1.0,
+            accum_out=T["r1"][:, 0:1])
+        mm([(sm[:, 64:65], T["BO"][:], T["r1"][:, 0:1], 1, 4)], [al("r1"), al("BO")], [("ms", 64, 65)])
+        act(T["r2"][:, 0:1], sm[:, 64:65], F.Identity, [("ms", 64, 65)], [al("r2")], 1, bias=255.6)
+        act(T["bnd"][:, v + 1:v + 2], sm[:, 64:65], F.Identity, [("ms", 64, 65), al("r2")], [("bnd", v + 1, v + 2)], 1,
+            bias=T["r2"][:, 0:1], scale=-1.0)
     return ops
 
 
@@ -441,6 +468,7 @@ def data_deps(ops):
         d = set(op["extra"])
         for name, lo, hi in op["rd"]:
             d.update(j for j, l2, h2, wr in hist.get(name, ()) if wr and l2 < hi and lo < h2)
+        op["raw"] = set(d)
         for name, lo, hi in op["wr"]:
             d.update(j for j, l2, h2, wr in hist.get(name, ()) if l2 < hi and lo < h2)
         d.discard(i)
@@ -466,20 +494,11 @@ def costs(ops, c):
             if k == "p":
                 t = n[0] * c["pe"] + n[1] * c["fp"]
             elif k == "g":
-                t = 150.0 + 2 * n * c["cyc"]
+                t = 170.0 + 2 * n * c["cyc"]
             else:
                 t = (c["fv"] if op["eng"] == "V" else c["fs"]) + n * c["cyc"] * (c["ga"] if k[1:] == "g" else c["sc"] if k == "vs" else 1.0)
             out.append((t, t))
     return out
-
-
-def tag_numbers(ops):
-    num = {}
-    return [num.setdefault(op["tag"], len(num)) for op in ops]
-
-
-def priorities(ops, tags, off, cfg):
-    return [-(max(op["visit"], 0) * cfg["PER"] + 10.0 * off[t]) for op, t in zip(ops, tags)]
 
 
 def schedule(ops, deps, cfg, c, seed):
@@ -494,9 +513,6 @@ def schedule(ops, deps, cfg, c, seed):
         prio[i] = cs[i][1] + max([prio[j] + c["lx"] for j in succ[i]] + [0.0])
     banks = [sorted(set(r[0] for r in op["rd"] + op["wr"] if r[0] in BANKS)) for op in ops]
     rng = np.random.default_rng(seed)
-    if cfg["OFF"]:
-        r = one_pass(ops, deps, succ, cs, priorities(ops, tag_numbers(ops), cfg["OFF"], cfg), cfg, c, banks)
-        return polish(ops, deps, succ, cs, banks, r[1], cfg, c, rng)
     best = None
     for k in range(cfg["FB"] + 1):
         r = one_pass(ops, deps, succ, cs, prio, cfg, c, banks)
@@ -577,7 +593,7 @@ def polish(ops, deps, succ, cs, banks, order, cfg, c, rng):
             return order
         return order[:a] + [i for i in mid if i not in take] + [i for i in mid if i in take] + order[b + 1:]
     cur = run(order)
-    best = (cur[0], order)
+    best = (cur[0], order, max(cur[1]))
     for k in range(cfg["POLISH"]):
         i = cur[1].index(max(cur[1]))
         arcs = []
@@ -612,14 +628,14 @@ def polish(ops, deps, succ, cs, banks, order, cfg, c, rng):
         if r[0] <= cur[0] - cfg["TEMP"] * (1.0 - k / cfg["POLISH"]) * float(np.log(rng.random() + 1e-12)):
             cur, order = r, new
             if r[0] < best[0]:
-                best = (r[0], new)
+                best = (r[0], new, max(r[1]))
     users, alld = {bk: {} for bk in BANKS}, [None] * n
     for i in best[1]:
         alld[i] = set(deps[i])
         for bk in banks[i]:
             alld[i].update(j for e2, j in users[bk].items() if e2 != eng[i])
             users[bk][eng[i]] = i
-    return best[0], best[1], alld
+    return best[2], best[1], alld
 
 
 def one_pass(ops, deps, succ, cs, prio, cfg, c, banks):
@@ -669,6 +685,199 @@ def one_pass(ops, deps, succ, cs, prio, cfg, c, banks):
     return max(fin), order, alld, fin
 
 
+def periodic(ops, deps, cfg, c, off=None, per=None):
+    n = len(ops)
+    cs = costs(ops, c)
+    succ = [set() for _ in range(n)]
+    for i in range(n):
+        for j in deps[i]:
+            succ[j].add(i)
+    eng = [op["eng"] for op in ops]
+    dl = [[(j, (0.0 if eng[i] == "P" else c["ls"]) if eng[i] == eng[j] and ops[j]["kind"] != "dma" else c["lx"])
+           for j in deps[i]] for i in range(n)]
+    banks = [sorted(set(r[0] for r in op["rd"] + op["wr"] if r[0] in BANKS)) for op in ops]
+    num = {}
+    tag = [num.setdefault(op["tag"], len(num)) for op in ops]
+    vis = [max(op["visit"], 0) for op in ops]
+    heads = [[i for i in range(n) if ops[i]["visit"] == v and ops[i]["tag"][3] == "Hu"] for v in range(NV)]
+    lx, dur, hold = c["lx"], [x[1] for x in cs], [x[0] for x in cs]
+    if off is None:
+        prio = [0.0] * n
+        for i in range(n - 1, -1, -1):
+            prio[i] = dur[i] + max([prio[j] + lx for j in succ[i]] + [0.0])
+        best = None
+        for k in range(cfg["FB"] + 1):
+            r = one_pass(ops, deps, succ, cs, prio, cfg, c, banks)
+            if best is None or r[0] < best[0]:
+                best = r
+            prio = one_pass(ops, succ, deps, cs, r[3], cfg, c, banks)[3]
+        fin = best[3]
+        hu = [min(fin[i] for i in h) for h in heads]
+        per, off = (hu[-1] - hu[1]) / (NV - 2), [0.0] * len(num)
+        for v in (-1, NV - 1, 2):
+            for i in range(n):
+                if ops[i]["visit"] == v:
+                    off[tag[i]] = fin[i] - dur[i] - (hu[v] - hu[0] if v >= 0 else 0.0)
+
+    def run(off):
+        pr = [vis[i] * per + off[tag[i]] for i in range(n)]
+        for i in range(n):
+            for j in deps[i]:
+                if pr[j] > pr[i]:
+                    pr[i] = pr[j]
+        order = sorted(range(n), key=lambda i: (pr[i], i))
+        free, users, fin, why = {}, {bk: {} for bk in BANKS}, [0.0] * n, [-1] * n
+        for i in order:
+            en = eng[i]
+            t, w = free.get(en, (0.0, -1))
+            for j, l in dl[i]:
+                if fin[j] + l > t:
+                    t, w = fin[j] + l, j
+            for bk in banks[i]:
+                u = users[bk]
+                for e2, j in u.items():
+                    if e2 != en and fin[j] + lx > t:
+                        t, w = fin[j] + lx, j
+                u[en] = i
+            fin[i], why[i] = t + dur[i], w
+            if en:
+                free[en] = (t + hold[i], i)
+        return max(fin) + cfg["SEC"] * sum(fin) / n, fin, why, order, pr
+    rng = np.random.default_rng(cfg["SEED"])
+    cur = best = run(off)
+    boff = off
+    for k in range(cfg["ANNEAL"]):
+        new, fin, why, pr, x = off[:], cur[1], cur[2], cur[4], rng.random()
+        if x < 0.6:
+            i, arcs = fin.index(max(fin)), []
+            while why[i] >= 0:
+                if why[i] not in deps[i]:
+                    arcs.append((why[i], i))
+                i = why[i]
+            if not arcs:
+                break
+            u, v = arcs[int(rng.integers(0, len(arcs)))]
+            if rng.random() < 0.5:
+                lim, st = pr[u] - 1 - float(rng.random()) * 300, [v]
+                while st:
+                    a = st.pop()
+                    if vis[a] * per + new[tag[a]] > lim or pr[a] > lim and a == v:
+                        new[tag[a]] = min(new[tag[a]], lim - vis[a] * per)
+                    st.extend(j for j in deps[a] if pr[j] > lim)
+            else:
+                new[tag[u]] = pr[v] + 1 + float(rng.random()) * 600 - vis[u] * per
+        elif x < 0.95:
+            for _ in range(int(rng.integers(1, 3))):
+                new[int(rng.integers(0, len(off)))] += float(rng.normal()) * (500 if rng.random() < 0.6 else 2500)
+        else:
+            v = int(rng.integers(1, NV - 1))
+            s0 = min(fin[i] - dur[i] - off[tag[i]] for i in heads[v])
+            for i in range(n):
+                if ops[i]["visit"] == v:
+                    new[tag[i]] = fin[i] - dur[i] - s0
+        r = run(new)
+        if r[0] <= cur[0] - cfg["TEMP"] * (1.0 - k / cfg["ANNEAL"]) * float(np.log(rng.random() + 1e-12)):
+            cur, off = r, new
+            if r[0] < best[0]:
+                best, boff = r, new
+    users, alld = {bk: {} for bk in BANKS}, [None] * n
+    for i in best[3]:
+        alld[i] = set(deps[i])
+        for bk in banks[i]:
+            alld[i].update(j for e2, j in users[bk].items() if e2 != eng[i])
+            users[bk][eng[i]] = i
+    return max(best[1]), best[3], alld, boff, per
+
+
+def names(ops):
+    out, seen = [], {}
+    for op in ops:
+        nm, lo = (op["wr"] + op["rd"])[0][:2]
+        lo = lo % L if nm in ("Tu", "ci", "co", "T2u") else lo % 16 * 16 if nm in ("bu", "bo") else 0 if nm == "bnd" else lo
+        k = "%s.%s.%d" % (op["eng"] or "R", nm[0] if nm[0] in "Xd" and len(nm) == 2 else nm, lo)
+        s = seen[op["visit"], k] = seen.get((op["visit"], k), 0) + 1
+        out.append(k + ("#%d" % s if s > 1 else ""))
+    return out
+
+
+def arrange(ops, deps, c):
+    n = len(ops)
+    cs = costs(ops, c)
+    eng = [op["eng"] for op in ops]
+    banks = [sorted(set(r[0] for r in op["rd"] + op["wr"] if r[0] in BANKS)) for op in ops]
+    pre = [[(j, (0.0 if eng[i] == "P" else c["ls"]) if eng[i] == eng[j] and ops[j]["kind"] != "dma" else c["lx"])
+            for j in sorted(deps[i])] for i in range(n)]
+    idx = {(op["visit"], k): i for i, (op, k) in enumerate(zip(ops, names(ops)))}
+    for e, seq in ORDER.items():
+        chain = [idx.get((v + w.count("+") - w.count("-"), e + "." + w.rstrip("+-")))
+                 for v in range(-1, NV + 1) for w in seq.split() if v + w.count("+") - w.count("-") >= 0]
+        chain = [i for i in chain if i is not None]
+        for a, b in zip(chain[:-1], chain[1:]):
+            if a not in deps[b]:
+                pre[b].append((a, 0.0))
+    suc = [[] for _ in range(n)]
+    for i in range(n):
+        for j, l in pre[i]:
+            suc[j].append((i, l))
+    left = [len(p) for p in pre]
+    topo = [i for i in range(n) if not left[i]]
+    for i in topo:
+        for j, l in suc[i]:
+            left[j] -= 1
+            if not left[j]:
+                topo.append(j)
+    tail = [0.0] * n
+    for i in topo[::-1]:
+        tail[i] = cs[i][1] + max([tail[j] + l for j, l in suc[i]] + [0.0])
+    best = None
+    for slack in (50.0, 100.0, 200.0, 300.0, 400.0, 600.0):
+        left = [len(p) for p in pre]
+        ready = [i for i in range(n) if not left[i]]
+        free, users, order, alld = {}, {bk: {} for bk in BANKS}, [], [None] * n
+        fin, base, est = [0.0] * n, [0.0] * n, [0.0] * n
+        while ready:
+            for i in ready:
+                est[i] = max([base[i], free.get(eng[i], 0.0)]
+                             + [fin[j] + c["lx"] for bk in banks[i] for en, j in users[bk].items() if en != eng[i]])
+            i0 = min(ready, key=lambda k: est[k])
+            i = max((k for k in ready if eng[k] == eng[i0] and est[k] <= est[i0] + slack), key=lambda k: tail[k])
+            alld[i] = set(deps[i])
+            for bk in banks[i]:
+                alld[i].update(j for en, j in users[bk].items() if en != eng[i])
+                users[bk][eng[i]] = i
+            fin[i] = est[i] + cs[i][1]
+            if eng[i]:
+                free[eng[i]] = est[i] + cs[i][0]
+            order.append(i)
+            ready.remove(i)
+            for j, l in suc[i]:
+                left[j] -= 1
+                if not left[j]:
+                    base[j] = max(fin[k] + l2 for k, l2 in pre[j])
+                    ready.append(j)
+        if best is None or max(fin) < best[0]:
+            best = (max(fin), order, alld)
+    return best
+
+
+ORDER = {
+    "V": "Hu.128 wI.0- bI.0- c1.192 c1.128 tk.192 u.192 Hu.0 tk.128 T1u.192 u.128 c1.64 T1u.128 c1.0 tk.64 u.64 mn.128 T1u.64 "
+         "tk.0 a1.128 u.0 qI.128 nI.128 T1u.0 nu.128 mx.128 E.0 E.1 mn.0 mx.0 a0.128 rel.128 qI.0 nI.0 sg0.128 sg1.128 sg2.128 "
+         "sg3.128 nu.0 uI.0 o1.0 uA.0 nr.128 jI.0 a1.256 T2.128 tt.0 tt.0#2 kT.128 ks.128 tt.0#3 kI.128 rel.0 kA.128 tt.0#4 "
+         "klo.128 w.128 sg1.0 sg0.0 sg2.0 wI.128 s8i.0 bI.128 sg3.0 X.0 nr.0 a0.256 T2.0 tt.0#5 tt.0#6 tt.0#7 kT.0 ks.0 kI.0 "
+         "kA.0 klo.0 w.0 tt.0#8",
+    "S": "x.192 r1.0- x.128 brC.128 r2.0- bnd.0- x.64 x.0 z.192 z.128 sC.0 brC.0 FB.0 z.64 z.0 e.192 e.128 hh.128 ab0.128 "
+         "ab1.128 ab2.128 ab3.128 e.0 e.64 s8.0 ab0.0 hh.0 ab1.0 ab2.0 ab3.0",
+}
+
+
+def close_groups(ops, order):
+    final = {ops[i]["group"]: i for i in order if "group" in ops[i]}
+    for i, op in enumerate(ops):
+        if "group" in op:
+            op["stop"][0] = final[op["group"]] == i
+
+
 PLAN = {}
 
 
@@ -680,8 +889,11 @@ def rank_program(g, core, T, topo):
     ops = build(g, T, topo.addr(nxt)[:2], topo.engines(core, nxt), CFG)
     if not PLAN:
         deps = data_deps(ops)
-        PLAN["p"] = schedule(ops, deps, CFG, COST, CFG["SEED"])
-    order, deps = PLAN["p"][1:]
+        PLAN["p"] = arrange(ops, deps, COST)
+        PLAN["raw"] = [op["raw"] for op in ops]
+    order, deps = PLAN["p"][1:3]
+    raw = PLAN["raw"]
+    close_groups(ops, order)
     q = {"V": g.vector, "S": g.scalar, "P": g.tensor, "G": g, "Y": g.sync}
     known = {k: {} for k in q}
     count = {k: 0 for k in "VSPG"}
@@ -696,6 +908,8 @@ def rank_program(g, core, T, topo):
         need = {}
         for j in deps[i]:
             if en == "P" and ops[j]["eng"] == "P":
+                continue
+            if CFG["WAW"] and en in "VS" and ops[j]["eng"] == en and ops[j]["kind"] != "dma" and j not in raw[i]:
                 continue
             if j in token and token[j][1] > need.get(token[j][0], (0, 0))[0]:
                 need[token[j][0]] = (token[j][1], j)

import numpy as np
from concourse.bass import DstId, RemoteDMATransfer
from concourse.mybir import AluOpType as A, ActivationFunctionType as F

CFG = dict(
    PX=[0, 64, 128, 192, 256],
    XV=[],
    P1=[0, 64, 128, 192, 256],
    P2=[0, 128, 256],
    P3=[0, 128, 256],
    PT=[0, 128, 256],
    P4=[0, 128, 256],
    CV="",
    NSQ={0: 0, 128: 0},
    WAW=0, S8=1, HS=1, FS=1,
    SGAT={0: 0, 64: 0, 128: 2, 192: 0},
    BK=128, PH=[0, 128, 256], PM=[0, 128, 256], PC=[0, 128, 256],
    G=64,
    SEED=0, SLACK=150.0, FB=3, ITER=60, STEP=3000.0, POLISH=3000, ANNEAL=8000, TEMP=200.0, FREE=0.4, SEC=0.1, FAR=0.2, ALL=0.5,
)
COST = dict(cyc=1.0, fv=55.0, fs=70.0, ga=1.5, sc=3.8, pe=0.52, fp=10.0, lx=120.0, ls=70.0,
            rl=3000.0, rb=0.03, ri=900.0, dl=2000.0, db=0.005)
NV, L, W, B = 5, 256, 4096, 1024
f32, bf, i32, u16 = "float32", "bfloat16", "int32", "uint16"


def sb(n, d):
    return ("sbuf", [128] + (n if isinstance(n, list) else [n]), d)


SCRATCH = {
    "X0": sb(W + 16, bf), "X1": sb(W + 16, bf), "tti": sb(B, i32), "tt": sb(B + L, f32), "tri": sb(L, i32),
    "sli": sb(16, i32),
    "Tu": sb(NV * L, u16), "ci": sb(NV * L, bf), "bu": sb(NV * 16, u16),
    "T2u": sb(NV * L, u16), "co": sb(NV * L, bf), "bo": sb(NV * 16, u16),
    "Tf": sb(L, f32), "T2": sb(L, f32), "bI": sb(16, i32), "ys": sb(16, f32), "bfl": sb(16, f32), "sC": sb(16, f32),
    "off": sb(16, u16),
    "x": sb(W, bf), "c1": sb(W, bf), "z": sb(W, bf), "mn": sb(W, bf), "mx": sb(W, bf),
    "e": sb(W, bf), "ab": sb(W, bf), "sg": sb(W, bf),
    "Hu": sb(L, u16), "Hf": sb(L, f32), "tk": sb(L, bf), "u": sb(L, f32), "T1u": sb(L, u16), "T1": sb(L, f32),
    "qI": sb(L, i32), "nI": sb(L, i32), "nf": sb(L, f32), "nu": sb(L, u16), "hh": sb(L, bf), "nr": sb(L, bf),
    "kT": sb(L, f32), "ks": sb(L, f32), "kI": sb(32, i32), "kA": sb(32, i32), "klo": sb(16, f32),
    "w": sb(16, f32), "FB": sb(16, f32), "wI": sb(16, i32), "nh": sb(16, bf),
    "r1": sb(8, f32), "r2": sb(8, bf), "bnd": sb(8, f32),
    "brC": sb(L, f32), "CLi": sb(32, i32), "CL": sb(32, u16), "E": sb(2 * L, bf), "o1": sb(16, f32),
    "uI": sb(16, i32), "uA": sb(16, i32), "jI": sb(16, i32), "ju": sb(16, u16), "s8": sb(L, f32), "s8i": sb(L, i32),
    "pI": sb(8, i32), "col": sb(24, f32), "J": sb(160, f32), "Jg": sb(128, f32), "Jr": sb([16, 8], f32),
    "Jh": sb([16, 8], f32), "t1": sb([16, 8], bf), "t2": sb([16, 8], bf), "J16": sb(16, f32),
    "IOT": sb(B, f32), "C4": sb(B, f32), "L16": sb(16, f32), "LD": sb(16, f32),
    "I": sb(128, bf), "nI_": sb(128, bf), "Ih": sb(128, bf), "I16": sb(128, bf), "rel": sb(L, bf), "NH": sb(128, bf),
    "NK": sb(128, bf), "If": sb(128, f32), "nIf": sb(128, f32),
    "CKa": sb(128, bf), "CKb": sb(128, bf), "CK": sb(128, bf), "BO": sb(128, f32),
    "W1": sb(144, bf), "W8": sb(144, bf), "Wh": sb(144, bf), "WI0": sb(160, f32), "WI1": sb(160, f32),
    "SLT": sb([16, 144], bf), "rmin": sb(2048, bf), "rmax": sb(2048, bf), "rk": sb(L, bf), "ones": sb(128, bf),
    "a0": ("psum", [128, 512], f32), "a1": ("psum", [128, 512], f32),
    "a2": ("psum", [128, 512], f32), "kp": ("psum", [128, 512], f32), "ms": ("psum", [128, 512], f32),
    "d0": ("psum", [128, 512], f32), "d1": ("psum", [128, 512], f32), "a3": ("psum", [128, 512], f32),
}
BANKS = ("a0", "a1", "a2", "kp", "ms", "d0", "d1", "a3")
SEMAPHORES = (["V", "S", "P", "G", "sent"] + ["dm%d" % i for i in range(20)]
              + ["%s%d_%d" % (k, v, c) for k in "tbc" for v in range(1, NV) for c in range(0, L, 32)])


def pieces(p):
    return list(zip(p[:-1], p[1:]))[::-1]


def classes(n):
    return 4 if n > 64 else 2 if n > 32 else 1


def build(g, T, dst, engines, cfg):
    ops = []
    V, S, P = g.vector, g.scalar, g.tensor
    mask = sum(1 << e for e in engines)
    visit, seen, opened = [-1], {}, {}
    BK = cfg["BK"]
    DB = ["d0", "d1"] + (["a3"] if BK == 128 else [])

    def add(eng, fn, rd, wr, kind, n, extra=(), sem=None, cnt=0):
        tag = (visit[0], eng, kind, (wr + rd)[0][0].rstrip("0123456789"))
        seen[tag] = seen.get(tag, 0) + 1
        ops.append(dict(eng=eng, fn=fn, rd=rd, wr=wr, kind=kind, n=n, extra=list(extra), sem=sem, cnt=cnt, visit=visit[0],
                        tag=(visit[0] < 0,) + tag[1:] + (seen[tag],)))
        return len(ops) - 1

    def vop(fn, rd, wr, n, m=1.0):
        return add("V", fn, rd, wr, "v", max(64.0, n * m))

    def ts(out, in0, s1, s2, o0, o1, rd, wr, n, m=1.0):
        if o1 is None:
            return vop(lambda: V.tensor_scalar(out, in0, s1, None, o0), rd, wr, n, m)
        return vop(lambda: V.tensor_scalar(out, in0, s1, s2, o0, o1), rd, wr, n, m)

    def tt(out, a, b, o, rd, wr, n, m=1.0):
        return vop(lambda: V.tensor_tensor(out, a, b, o), rd, wr, n, m)

    def cp(out, a, rd, wr, n, m=1.0):
        return vop(lambda: V.tensor_copy(out, a), rd, wr, n, m)

    def gc_(out, a, rd, wr, n):
        return add("G", lambda: g.affine_select(out, a, [[0, n]], A.is_ge, 0.0, 0, 0), rd, wr, "g", n)

    def cvt(key, out, a, rd, wr, n):
        return (cp if key in cfg["CV"] else gc_)(out, a, rd, wr, n)

    def ms(out, c, wr, n):
        return vop(lambda: V.memset(out, c), [], wr, n, 0.5)

    def gtt(out, a, b, o, rd, wr, n):
        return add("V", lambda: V.tensor_tensor(out, a, b, o), rd, wr, "vg", n)

    def gcp(out, a, rd, wr, n, kind="vg"):
        return add("V", lambda: V.tensor_copy(out, a), rd, wr, kind, n)

    def act(out, a, fn, rd, wr, n, kind="s", **kw):
        return add("S", lambda: S.activation(out, a, fn, **kw), rd, wr, kind, n)

    def mm(lst, rd, wr, start=True):
        stop = [True]

        def go():
            r = None
            for k, t in enumerate(lst):
                r = P.matmul(t[0], t[1], t[2], start and k == 0, stop[0] and k == len(lst) - 1)
            return r
        i = add("P", go, rd, wr, "p", (sum(max(64, t[3]) * t[4] for t in lst), len(lst)))
        bank = [r[0] for r in wr + rd if r[0] in BANKS][0]
        if start:
            opened[bank] = i
        ops[i].update(stop=stop, group=opened[bank])
        return i

    ndma = [0]

    def dma(q, out, a, rd, wr, nbytes):
        e = g.sync if q == "Y" else g.scalar
        ndma[0] += 1
        return add(q, lambda: e.dma_start(out, a), rd, wr, "dma", nbytes, sem="dm%d" % (ndma[0] - 1), cnt=16)

    def send(src, to, sem, rd, land, nbytes):
        s = add("G", lambda: g.remote_dma(to, src, T.sem[sem], T.sem["sent"], dst[1], dst[0], mask), rd, [], "send", 0,
                cnt=len(engines))
        add(None, None, [], [land], "recv", 128 * nbytes, extra=[s], sem=sem, cnt=len(engines))

    def al(n):
        return (n, 0, 1 << 20)

    def iota(out, pat, base, cm, wr, n, flt=True):
        if flt:
            return add("G", lambda: g.iota(out, pat, base, cm, allow_small_or_imprecise_dtypes=True), [], wr, "g", n)
        return add("G", lambda: g.iota(out, pat, base, cm), [], wr, "g", n)

    dma("Y", T["tri"][:], T.trav[:], [], [al("tri")], 131072)
    dma("S", T["sli"][:], T.slot[:], [], [al("sli")], 8192)
    dma("Y", T["X0"][:, 0:W], T.clk[:], [], [("X0", 0, W)], 1179648)
    dma("Y", T["tti"][:], T.ttab[:], [], [al("tti")], 1703936)
    dma("Y", T["ci"][:, 0:L], T.last[:], [], [("ci", 0, L)], 1769472)

    pI, col, J = T["pI"], T["col"], T["J"]
    iota(pI[:, 0:1], [[1, 1]], 0, 1, [("pI", 0, 1)], 1, False)
    iota(J[:], [[1, 160]], 0, 0, [al("J")], 160)
    iota(T["J16"][:], [[16, 16]], 0, 0, [al("J16")], 16)
    iota(T["IOT"][:], [[1, B]], 0, 0, [al("IOT")], B)
    iota(T["Jr"][:], [[1, 16], [0, 8]], 0, 0, [al("Jr")], 128)
    iota(T["Jh"][:], [[0, 16], [1, 8]], 0, 0, [al("Jh")], 128)
    iota(T["Jg"][:], [[1, 8], [0, 16]], 0, 0, [al("Jg")], 128)

    def pc(k):
        return pI[:, k:k + 1]

    def cc(k):
        return col[:, k:k + 1]

    def rp(k):
        return ("pI", k, k + 1)

    def rc(k):
        return ("col", k, k + 1)
    ts(pc(1), pc(0), 15, None, A.bitwise_and, None, [rp(0)], [rp(1)], 1)
    ts(pc(2), pc(0), 4, None, A.arith_shift_right, None, [rp(0)], [rp(2)], 1)
    ts(pc(3), pc(0), 4, 1, A.arith_shift_right, A.bitwise_and, [rp(0)], [rp(3)], 1)
    ts(pc(4), pc(0), 7, None, A.bitwise_and, None, [rp(0)], [rp(4)], 1)
    cp(col[:, 0:5], pI[:, 0:5], [("pI", 0, 5)], [("col", 0, 5)], 5)
    ts(cc(13), cc(0), 16.0, None, A.add, None, [rc(0)], [rc(13)], 1)
    ts(cc(6), cc(2), 16.0, 15.0, A.mult, A.add, [rc(2)], [rc(6)], 1)
    ts(cc(7), cc(3), -1.0, 1.0, A.mult, A.add, [rc(3)], [rc(7)], 1)
    ts(cc(8), cc(4), -1024.0, 207.0 * 1024, A.mult, A.add, [rc(4)], [rc(8)], 1)
    ts(cc(9), cc(1), 2452.0, -0.25, A.mult, A.add, [rc(1)], [rc(9)], 1)
    ts(cc(12), cc(0), -1.0, 127.0, A.mult, A.add, [rc(0)], [rc(12)], 1)
    need = {}
    for a, b in pieces(cfg["P3"]):
        nc, nq = classes(b - a), cfg["NSQ"][a]
        if (nc, nq) not in need:
            k = need[nc, nq] = 14 + len(need)
            ts(pc(5), pc(0), nc - 1, None, A.bitwise_and, None, [rp(0)], [rp(5)], 1)
            ts(cc(10), pc(5), float(nc - nq), -8.0, A.is_ge, A.mult, [rp(5)], [rc(10)], 1)
            ts(cc(k), cc(10), 28.0, None, A.add, None, [rc(10)], [rc(k)], 1)
    for name, f in (("I", 1.0), ("nI_", -1.0), ("Ih", 0.5), ("I16", 16.0), ("NH", -1024.0),
                    ("NK", -2.0 ** 26), ("If", 1.0), ("nIf", -1.0)):
        ts(T[name][:], J[:, 0:128], cc(0), f, A.is_equal, A.mult, [al("J"), rc(0)], [al(name)], 128)
    ts(T["CKa"][:], J[:, 0:128], cc(0), cc(8), A.is_equal, A.mult, [al("J"), rc(0), rc(8)], [al("CKa")], 128)
    ts(T["CKb"][:], J[:, 0:128], cc(12), -2.0 ** 24, A.is_equal, A.mult, [al("J"), rc(12)], [al("CKb")], 128)
    tt(T["CK"][:], T["CKa"][:], T["CKb"][:], A.add, [al("CKa"), al("CKb")], [al("CK")], 128, 2)
    ts(T["BO"][:], T["Jg"][:], cc(2), None, A.is_equal, None, [al("Jg"), rc(2)], [al("BO")], 128)
    for name, f in (("W1", 1.0), ("W8", 8192.0), ("Wh", 0.5)):
        ts(T[name][:], J[:, 0:144], cc(6), f, A.is_equal, A.mult, [al("J"), rc(6)], [al(name)], 144)
    ts(T["WI0"][:], J[:], cc(13), cc(7), A.is_equal, A.mult, [al("J"), rc(13), rc(7)], [al("WI0")], 160)
    ts(T["WI1"][:], J[:], cc(13), cc(3), A.is_equal, A.mult, [al("J"), rc(13), rc(3)], [al("WI1")], 160)
    for r in range(0, 16, 4):
        iota(T["SLT"][:, r:r + 4, :], [[0, 4], [0, 144]], 0, 0, [("SLT", r, r + 4)], 576)
    ts(T["t1"][:], T["Jr"][:], cc(1), 8192.0, A.is_gt, A.mult, [al("Jr"), rc(1)], [al("t1")], 128)
    ts(T["t2"][:], T["Jh"][:], cc(2), None, A.is_equal, None, [al("Jh"), rc(2)], [al("t2")], 128)
    tt(T["SLT"][:, :, 15:143:16], T["t1"][:], T["t2"][:], A.mult, [al("t1"), al("t2")], [al("SLT")], 128, 2)
    nsc = 16 * max(b - a for a, b in pieces(cfg["PM"]))
    for s in range(0, 16 * max(b - a for a, b in pieces(cfg["P2"])), 512):
        iota(T["rmin"][:, s:s + 512], [[0, 32], [-256, 16]], 255, 0, [("rmin", s, s + 512)], 512)
    ms(T["rmax"][:, 0:nsc], 256.0, [al("rmax")], nsc)
    ms(T["rmax"][:, 0:nsc:16], 0.0, [al("rmax")], nsc // 16)
    ms(T["rk"][:], 0.0, [al("rk")], L)
    ms(T["rk"][:, 0:L:8], -2.0 ** 28, [al("rk")], 32)
    ms(T["ones"][:], 1.0, [al("ones")], 128)
    iota(T["CLi"][:, 0:16], [[1, 16]], 0, 0, [("CLi", 0, 16)], 16, False)
    iota(T["CLi"][:, 16:32], [[2, 8], [0, 2]], 0, 0, [("CLi", 16, 32)], 16, False)
    gc_(T["CL"][:], T["CLi"][:], [al("CLi")], [al("CL")], 32)
    ms(T["bnd"][:, 0:1], 256.0, [("bnd", 0, 1)], 1)
    act(T["C4"][:], T["IOT"][:], F.Identity, [al("IOT"), rc(9)], [al("C4")], B, bias=cc(9), scale=148.0)
    ts(T["LD"][:], T["J16"][:], cc(1), float(B), A.add, A.add, [al("J16"), rc(1)], [al("LD")], 16)
    ts(T["L16"][:], T["J16"][:], cc(1), 16.0, A.add, A.mult, [al("J16"), rc(1)], [al("L16")], 16)
    cp(T["bu"][:, 0:16], T["sli"][:], [al("sli")], [("bu", 0, 16)], 16)
    cp(T["Tu"][:, 0:L], T["tri"][:], [al("tri")], [("Tu", 0, L)], L)
    for s in range(0, B, 256):
        gc_(T["tt"][:, s:s + 256], T["tti"][:, s:s + 256], [al("tti")], [("tt", s, s + 256)], 256)

    def sel(name, k):
        return T[name][:, 15 - k:143 - k]

    def reg(r, a, b):
        bank, s = "a%d" % (a // BK), BK * r + a % BK
        return T[bank][:, s:s + b - a], (bank, s, s + b - a), al("g" + bank)

    tab, kp, sm = T["tt"], T["kp"], T["ms"]
    e, mn, mx = T["e"], T["mn"], T["mx"]
    I, If, nIf, ones = T["I"][:], T["If"][:], T["nIf"][:], T["ones"]
    dturn = [0]

    def dbank():
        dturn[0] += 1
        return DB[dturn[0] % len(DB)]

    def cut(a, b):
        return [(s, min(b, s + cfg["G"])) for s in range(a, b, cfg["G"])][::-1]
    for v in range(NV):
        visit[0] = v
        last = v == NV - 1
        o, ob = v * L, v * 16
        xn, xo = "X%d" % (v % 2), "X%d" % (1 - v % 2)
        X = T[xn]
        dma("Y", T[xo][:, 0:W], X[:, 0:W], [(xn, 0, W), ("bu", ob, ob + 16), ("ci", o, o + L)], [(xo, 0, W)], 1048576)
        for a, b in pieces(cfg["PX"]):
            win, rd = X[:, 0:W].indirect(T["Tu"][:, o + a:o + b]), [al(xn), ("Tu", o + a, o + b)]
            if a in cfg["XV"]:
                gcp(T["x"][:, 16 * a:16 * b], win, rd, [("x", a, b)], 16 * (b - a))
            else:
                act(T["x"][:, 16 * a:16 * b], win, F.Copy, rd, [("x", a, b)], 16 * (b - a), "sg")
        for a, b in pieces([0, 128, 256]):
            gc_(T["Tf"][:, a:b], T["Tu"][:, o + a:o + b], [("Tu", o + a, o + b)], [("Tf", a, b)], b - a)
            bl, rbl = T["bu"][:, ob + a // 16:ob + b // 16], ("bu", ob + a // 16, ob + b // 16)
            act(T["brC"][:, a:b], T["C4"][:, 0:B].indirect(bl), F.Copy, [al("C4"), rbl], [("brC", a, b)], b - a, "sg")
        for a, b in pieces(cfg["P1"]):
            n = b - a
            bl, rbl = T["bu"][:, ob + a // 16:ob + b // 16], ("bu", ob + a // 16, ob + b // 16)
            tn = "tt" if v else "tti"
            (p0, r0, gr), (p1, r1, _), (p2, r2, _) = reg(0, a, b), reg(1, a, b), reg(2, a, b)
            if b in cfg["PH"]:
                ah = cfg["PH"][cfg["PH"].index(b) - 1]
                gcp(T["Hu"][:, ah:b], T[tn][:, 0:B].indirect(T["bu"][:, ob + ah // 16:ob + b // 16]),
                    [al(tn), ("bu", ob + ah // 16, ob + b // 16)], [("Hu", ah, b)], b - ah)
                gc_(T["Hf"][:, ah:b], T["Hu"][:, ah:b], [("Hu", ah, b)], [("Hf", ah, b)], b - ah)
            mm([(p1, If, T["Hf"][:, a:b], n, 4), (p1, nIf, T["Tf"][:, a:b], n, 4)],
               [("Hf", a, b), ("Tf", a, b), al("If"), al("nIf"), gr], [r1])
            for a2, b2 in cut(a, b):
                gtt(T["c1"][:, 16 * a2:16 * b2], X[:, 0:W].indirect(T["Hu"][:, a2:b2]), T["x"][:, 16 * a2:16 * b2], A.is_ge,
                    [al(xn), ("Hu", a2, b2), ("x", a2, b2)], [("c1", a2, b2)], 16 * (b2 - a2))
            p0, r0, gr0 = reg(3, a ^ 128, (a ^ 128) + n) if BK == 128 else reg(0, a, b)
            mm([(p0, sel("W1", k), T["c1"][:, 16 * a + k:16 * b:16], n, 1) for k in range(16)], [("c1", a, b), al("W1"), gr0], [r0])
            ts(T["tk"][:, a:b], p0, T["bnd"][:, v:v + 1], 265.0, A.add, A.is_ge, [r0, ("bnd", v, v + 1)], [("tk", a, b)], n)
            tt(T["u"][:, a:b], p1, T["tk"][:, a:b], A.mult, [r1, ("tk", a, b)], [("u", a, b)], n)
            mm([(p2, If, T["Tf"][:, a:b], n, 4), (p2, If, T["u"][:, a:b], n, 4)], [("u", a, b), ("Tf", a, b), al("If"), gr], [r2])
            cp(T["T1u"][:, a:b], p2, [r2], [("T1u", a, b)], n)
            gc_(T["T1"][:, a:b], T["T1u"][:, a:b], [("T1u", a, b)], [("T1", a, b)], n)
            for a2, b2 in cut(a, b):
                act(T["z"][:, 16 * a2:16 * b2], X[:, 0:W].indirect(T["T1u"][:, a2:b2]), F.Copy,
                    [al(xn), ("T1u", a2, b2)], [("z", a2, b2)], 16 * (b2 - a2), "sg")
        for a, b in pieces(cfg["P2"]):
            n = b - a
            zz = T["z"][:, 16 * a:16 * b]
            vop(lambda a=a, b=b, n=n, zz=zz: V.tensor_tensor_scan(mn[:, 16 * a:16 * b], T["rmin"][:, 0:16 * n], zz, 0.0, A.max, A.min),
                [("z", a, b), al("rmin")], [("mn", a, b)], 16 * n, 0.5)
            if a in cfg["PM"]:
                bm = cfg["PM"][cfg["PM"].index(a) + 1]
                vop(lambda a=a, b=bm: V.tensor_tensor_scan(mx[:, 16 * a:16 * b], T["rmax"][:, 0:16 * (b - a)], T["z"][:, 16 * a:16 * b],
                                                           0.0, A.min, A.max), [("z", a, bm), al("rmax")], [("mx", a, bm)], 16 * (bm - a), 0.5)
            m, rm = mn[:, 16 * a + 15:16 * b:16], ("mn", a, b)
            (p0, r0, gr), (p1, r1, _), (p2, r2, _) = reg(0, a, b), reg(1, a, b), reg(2, a, b)
            mm([(p0, I, m, n, 1), (p0, T["Ih"][:], ones[:, 0:n], n, 1)], [rm, al("I"), al("Ih"), al("ones"), gr], [r0])
            tt(p1, p0, T["T1"][:, a:b], A.mult, [r0, ("T1", a, b)], [r1], n)
            tt(T["qI"][:, a:b], p1, T["brC"][:, a:b], A.add, [r1, ("brC", a, b)], [("qI", a, b)], n)
            ts(T["nI"][:, a:b], T["qI"][:, a:b], 2, W - 1, A.arith_shift_right, A.bitwise_and, [("qI", a, b)], [("nI", a, b)], n)
            cp(T["nu"][:, a:b], T["nI"][:, a:b], [("nI", a, b)], [("nu", a, b)], n)
            gc_(T["nf"][:, a:b], T["nI"][:, a:b], [("nI", a, b)], [("nf", a, b)], n)
            if a in cfg["PC"]:
                bm = cfg["PC"][cfg["PC"].index(a) + 1]
                gc_(T["co"][:, o + a:o + bm], mn[:, 16 * a + 15:16 * bm:16], [("mn", a, bm)], [("co", o + a, o + bm)], bm - a)
                hb = 192.0 - 511.5 / 1024
                if cfg["HS"]:
                    act(T["hh"][:, a:bm], T["nf"][:, a:bm], F.Identity, [("nf", a, bm)], [("hh", a, bm)], bm - a, bias=hb, scale=1.0 / 1024)
                else:
                    ts(T["hh"][:, a:bm], T["nu"][:, a:bm], 1.0 / 1024, hb, A.mult, A.add, [("nu", a, bm)], [("hh", a, bm)], bm - a, 0.5)
            mm([(p2, If, T["T1"][:, a:b], n, 4), (p2, nIf, T["nf"][:, a:b], n, 4)],
               [("T1", a, b), ("nf", a, b), al("If"), al("nIf"), gr], [r2])
        if last:
            dma("Y", T.ylast[:], T["co"][:, o:o + L], [("co", o, o + L)], [], 65536)
        else:
            send(T["co"][:, o:o + L], T["ci"][:, o + L:o + 2 * L], "c%d_0" % (v + 1), [("co", o, o + L)],
                 ("ci", o + L, o + 2 * L), 2 * L)
        mm([(sm[:, 0:16], sel("W1", r), mx[:, 16 * r + 15:W:256], 16, 1) for r in range(16)], [al("mx"), al("W1")], [("ms", 0, 16)])
        cp(T["uI"][:], sm[:, 0:16], [("ms", 0, 16)], [al("uI")], 16)
        ts(T["uA"][:], T["uI"][:], 15, None, A.bitwise_and, None, [al("uI")], [al("uA")], 16)
        tt(T["jI"][:], T["uA"][:], T["L16"][:], A.add, [al("uA"), al("L16")], [al("jI")], 16)
        gc_(T["ju"][:], T["jI"][:], [al("jI")], [al("ju")], 16)
        if cfg["S8"]:
            act(T["s8"][:], X[:, 0:W].indirect(T["ju"][:]), F.Identity, [al(xn), al("ju")], [al("s8")], L, "sg", bias=-0.25, scale=0.5)
            mm([(sm[:, L:2 * L], T["Ih"][:], mx[:, 15:W:16], L, 1)], [al("mx"), al("Ih")], [("ms", L, 2 * L)])
            tt(T["s8i"][:], sm[:, L:2 * L], T["s8"][:], A.add, [("ms", L, 2 * L), al("s8")], [al("s8i")], L)
        else:
            gtt(T["s8"][:], X[:, 0:W].indirect(T["ju"][:]), mx[:, 15:W:16], A.add, [al(xn), al("ju"), al("mx")], [al("s8")], L)
            ts(T["s8i"][:], T["s8"][:], 0.5, -0.25, A.mult, A.add, [al("s8")], [al("s8i")], L)
        gcp(T[xo][:, 0:W].indirect(T["ju"][:]), T["s8i"][:], [al("s8i"), al("ju")], [(xo, 0, W)], L, "vs")
        if last:
            dma("Y", T.yclk[:], T[xo][:, 0:W], [(xo, 0, W)], [], 1048576)
        bl, rbl = T["bu"][:, ob:ob + 16], ("bu", ob, ob + 16)
        gc_(T["bfl"][:], bl, [rbl], [al("bfl")], 16)
        if cfg["FS"]:
            act(T["FB"][:], T["bfl"][:], F.Identity, [al("bfl")], [al("FB")], 16, bias=97.0 - 2 ** 24)
            act(T["sC"][:], T["bfl"][:], F.Identity, [al("bfl"), rc(9)], [al("sC")], 16, bias=cc(9), scale=148.0)
        else:
            ts(T["FB"][:], bl, 97.0 - 2 ** 24, None, A.add, None, [rbl], [al("FB")], 16)
            ts(T["sC"][:], bl, 148.0, cc(9), A.mult, A.add, [rbl, rc(9)], [al("sC")], 16)
        E = T["E"]
        for k in range(2):
            gtt(E[:, k * L:(k + 1) * L], T["sC"][:, 0:16].indirect(T["CL"][:, 16 * k:16 * k + 16]), T["brC"][:], A.is_equal,
                [al("sC"), al("CL"), al("brC")], [("E", k, k + 1)], L)
        lst = ([(sm[:, 16:32], If, T["bfl"][:], 16, 4)]
               + [(sm[:, 16:32], T["SLT"][:, r, 15 - r:143 - r], E[:, r:L:16], 16, 1) for r in range(16)]
               + [(sm[:, 17:32:2], sel("W8", r), E[:, L + 16 + r:2 * L:32], 8, 1) for r in range(16)])
        mm(lst, [al("E"), al("SLT"), al("W8"), al("bfl"), al("If")], [("ms", 16, 32)])
        tt(T["o1"][:], sm[:, 16:32], T["LD"][:], A.min, [("ms", 16, 32), al("LD")], [al("o1")], 16)
        gc_(T["off"][:], T["o1"][:], [al("o1")], [al("off")], 16)
        for a, b in pieces(cfg["P3"]):
            n, nsq = b - a, cfg["NSQ"][a]
            nc = classes(n)
            nr = 16 // nc
            for a2, b2 in cut(a, b):
                act(e[:, 16 * a2:16 * b2], X[:, 0:W].indirect(T["nu"][:, a2:b2]), F.Copy, [al(xn), ("nu", a2, b2)],
                    [("e", a2, b2)], 16 * (b2 - a2), "sg")
            M, m = mx[:, 16 * a + 15:16 * b:16], mn[:, 16 * a + 15:16 * b:16]

            def cls(t, q):
                return t[:, 16 * a + q:16 * b:nc]

            def diff(q, y, ry, fn, out, **kw):
                dn = dbank()
                mm([(T[dn][:, r:nr * n:nr], T["nI_"][:], y, n, 1) for r in range(nr)], [ry, al("nI_")], [al(dn), al("g" + dn)])
                mm([(T[dn][:, 0:nr * n], I, cls(e, q), nr * n, 1)], [("e", a, b), al("I"), al("g" + dn)], [al(dn)], False)
                act(cls(T[out], q), T[dn][:, 0:nr * n], fn, [al(dn)], [(out + str(q), a, b)], nr * n, **kw)
            (p0, r0, gr), (p2, r2, _) = reg(0, a, b), reg(2, a, b)
            todo = [("ab", q) for q in range(nc)]
            todo[cfg["SGAT"][a]:cfg["SGAT"][a]] = [("sg", q) for q in range(nc - nsq, nc)]
            for kind, q in todo:
                if kind == "ab":
                    diff(q, M, ("mx", a, b), F.Abs, "ab")
                else:
                    diff(q, m, ("mn", a, b), F.Sign, "sg", bias=0.5)
            if BK == 128:
                mr, m0, rmr, nv, gm = T["a2"], 0, al("a2"), nr, []
            else:
                mr, m0, rmr, nv, gm = T[r0[0]], 256, (r0[0], 256, 512), 4, [gr]
            mm([(mr[:, m0 + r:m0 + nv * n:nv], I, m, n, 1) for r in range(nv)], [("mn", a, b), al("I")] + gm, [rmr])
            tt(T["rel"][:, a:b], mr[:, m0:m0 + nv * n:nv], T["ci"][:, o + a:o + b], A.is_gt, [rmr, ("ci", o + a, o + b)],
               [("rel", a, b)], n)
            for q in range(nc - nsq):
                for s in range(q, 16 // nv, nc):
                    tt(T["sg"][:, 16 * a + s:16 * b:16 // nv], e[:, 16 * a + s:16 * b:16 // nv], mr[:, m0:m0 + nv * n], A.is_ge,
                       [("e", a, b), rmr], [("sg%d" % q, a, b)] if s == q else [("sh%d" % q, a, b)], nv * n)
            for q in range(nc):
                onv = q < nc - nsq
                mm([(p0, sel("W1" if onv else "Wh", p), T["sg"][:, 16 * a + p:16 * b:16], n, 1) for p in range(q, 16, nc)]
                   + ([] if q else [(p0, T["I16"][:], T["rel"][:, a:b], n, 1)]),
                   [("sg%d" % q, a, b), ("sh%d" % q, a, b), al("W1"), al("Wh"), al("I16"), ("rel", a, b)], [r0, gr], q == 0)
            kb = need[nc, nsq]
            ts(T["nr"][:, a:b], p0, cc(kb), None, A.is_lt, None, [r0, rc(kb)], [("nr", a, b)], n)
            tt(p2, p2, T["nr"][:, a:b], A.mult, [r2, ("nr", a, b)], [r2], n)
            tt(T["T2"][:, a:b], p2, T["nf"][:, a:b], A.add, [r2, ("nf", a, b)], [("T2", a, b)], n)
            if not last and a in cfg["PT"]:
                bt = cfg["PT"][cfg["PT"].index(a) + 1]
                cvt("t", T["T2u"][:, o + a:o + bt], T["T2"][:, a:bt], [("T2", a, bt)], [("T2u", o + a, o + bt)], bt - a)
                send(T["T2u"][:, o + a:o + bt], T["Tu"][:, o + L + a:o + L + bt], "t%d_%d" % (v + 1, a), [("T2u", o + a, o + bt)],
                     ("Tu", o + L + a, o + L + bt), 2 * (bt - a))
            for a5 in range(b - 32, a - 1, -32):
                gcp(tab[:, 0:B + L].indirect(T["off"][:, a5 // 16:a5 // 16 + 2]), T["T2"][:, a5:a5 + 32],
                    [("T2", a, b), al("off")], [al("tt")], 32, "vs")
            rk_ = [("kp", a, b), al("gk")]
            mm([(kp[:, a:b], T["CK"][:], ones[:, 0:n], n, 1), (kp[:, a:b], T["NH"][:], T["hh"][:, a:b], n, 1),
                (kp[:, a:b], If, T["nf"][:, a:b], n, 4)],
               [("hh", a, b), ("nf", a, b), al("CK"), al("NH"), al("If"), al("ones")], rk_)
            for q in range(nc):
                mm([(kp[:, a:b], sel("W8", p), T["ab"][:, 16 * a + p:16 * b:16], n, 1) for p in range(q, 16, nc)],
                   [("ab%d" % q, a, b), al("W8")] + rk_, [("k%d" % q, a, b)], False)
            mm([(kp[:, a:b], T["NK"][:], T["nr"][:, a:b], n, 1)], [("nr", a, b), al("NK")] + rk_, [("k4", a, b)], False)
            if a not in cfg["P4"]:
                continue
            b = cfg["P4"][cfg["P4"].index(a) + 1]
            n = b - a
            vop(lambda a=a, b=b: V.transpose(T["kT"][:, a:b], kp[:, a:b]), [("kp", a, b)] + [("k%d" % q, a, b) for q in range(5)],
                [("kT", a, b)], n)
            vop(lambda a=a, b=b, n=n: V.tensor_tensor_scan(T["ks"][:, a:b], T["rk"][:, 0:n], T["kT"][:, a:b], 0.0, A.add, A.max),
                [("kT", a, b), al("rk")], [("ks", a, b)], n)
            a8, b8, a6, b6 = a // 8, b // 8, a // 16, b // 16
            cp(T["kI"][:, a8:b8], T["ks"][:, a + 7:b:8], [("ks", a, b)], [("kI", a, b)], 16)
            ts(T["kA"][:, a8:b8], T["kI"][:, a8:b8], -7169, None, A.bitwise_and, None, [("kI", a, b)], [("kA", a, b)], 16)
            ts(T["klo"][:, a6:b6], T["kA"][:, a8:b8:2], 1024.0, None, A.add, None, [("kA", a, b)], [("klo", a, b)], 16)
            tt(T["w"][:, a6:b6], T["klo"][:, a6:b6], T["kA"][:, a8 + 1:b8:2], A.max, [("kA", a, b), ("klo", a, b)], [("w", a, b)], 16)
            lst = []
            for u in range(2):
                for h in range(2):
                    s0 = 16 - 16 * (h - u)
                    lst.append((sm[:, 32 + a6 + u:32 + b6:2], T["WI%d" % u][:, s0:s0 + 128], T["w"][:, a6 + h:b6:2], 8, 4))
            rw = ("ms", 32 + a6, 32 + b6)
            mm(lst, [("w", a, b), al("WI0"), al("WI1")], [rw])
            tt(T["wI"][:, a6:b6], sm[:, 32 + a6:32 + b6], T["FB"][:, a6:b6], A.max, [rw, al("FB")], [("wI", a, b)], 16)
            ts(T["bI"][:, a6:b6], T["wI"][:, a6:b6], B - 1, None, A.bitwise_and, None, [("wI", a, b)], [("bI", a, b)], 16)
            if last:
                gc_(T["ys"][:, a6:b6], T["bI"][:, a6:b6], [("bI", a, b)], [("ys", a, b)], b6 - a6)
            else:
                rb = ("bo", ob + a6, ob + b6)
                cvt("b", T["bo"][:, ob + a6:ob + b6], T["bI"][:, a6:b6], [("bI", a, b)], [rb], b6 - a6)
                send(T["bo"][:, ob + a6:ob + b6], T["bu"][:, ob + 16 + a6:ob + 16 + b6], "b%d_%d" % (v + 1, a), [rb],
                     ("bu", ob + 16 + a6, ob + 16 + b6), n // 8)
        if last:
            dma("Y", T.yttab[:], tab[:, 0:B], [al("tt")], [], 524288)
            dma("Y", T.ytrav[:], T["T2"][:], [al("T2")], [], 131072)
            dma("Y", T.yslot[:], T["ys"][:], [al("ys")], [], 8192)
            break
        mm([(sm[:, 48:64], sel("W1", r), T["nr"][:, r:L:16], 16, 1) for r in range(16)], [al("nr"), al("W1")], [("ms", 48, 64)])
        act(T["nh"][:], sm[:, 48:64], F.Sign, [("ms", 48, 64)], [al("r1"), al("nh")], 40, bias=16.0, scale=-1.0,
            accum_out=T["r1"][:, 0:1])
        mm([(sm[:, 64:65], T["BO"][:], T["r1"][:, 0:1], 1, 4)], [al("r1"), al("BO")], [("ms", 64, 65)])
        act(T["r2"][:, 0:1], sm[:, 64:65], F.Identity, [("ms", 64, 65)], [al("r2")], 1, bias=255.6)
        act(T["bnd"][:, v + 1:v + 2], sm[:, 64:65], F.Identity, [("ms", 64, 65), al("r2")], [("bnd", v + 1, v + 2)], 1,
            bias=T["r2"][:, 0:1], scale=-1.0)
    return ops


def data_deps(ops):
    hist, deps = {}, []
    for i, op in enumerate(ops):
        d = set(op["extra"])
        for name, lo, hi in op["rd"]:
            d.update(j for j, l2, h2, wr in hist.get(name, ()) if wr and l2 < hi and lo < h2)
        op["raw"] = set(d)
        for name, lo, hi in op["wr"]:
            d.update(j for j, l2, h2, wr in hist.get(name, ()) if l2 < hi and lo < h2)
        d.discard(i)
        deps.append(d)
        for name, lo, hi in op["rd"]:
            hist.setdefault(name, []).append((i, lo, hi, False))
        for name, lo, hi in op["wr"]:
            hist[name] = [t for t in hist.get(name, []) if not (lo <= t[1] and t[2] <= hi)] + [(i, lo, hi, True)]
    return deps


def costs(ops, c):
    out = []
    for op in ops:
        k, n = op["kind"], op["n"]
        if k == "dma":
            out.append((100.0, c["dl"] + n * c["db"]))
        elif k == "send":
            out.append((c["ri"], c["ri"]))
        elif k == "recv":
            out.append((0.0, c["rl"] - c["ri"] + n * c["rb"]))
        else:
            if k == "p":
                t = n[0] * c["pe"] + n[1] * c["fp"]
            elif k == "g":
                t = 170.0 + 2 * n * c["cyc"]
            else:
                t = (c["fv"] if op["eng"] == "V" else c["fs"]) + n * c["cyc"] * (c["ga"] if k[1:] == "g" else c["sc"] if k == "vs" else 1.0)
            out.append((t, t))
    return out


def schedule(ops, deps, cfg, c, seed):
    n = len(ops)
    cs = costs(ops, c)
    succ = [set() for _ in range(n)]
    for i in range(n):
        for j in deps[i]:
            succ[j].add(i)
    prio = [0.0] * n
    for i in range(n - 1, -1, -1):
        prio[i] = cs[i][1] + max([prio[j] + c["lx"] for j in succ[i]] + [0.0])
    banks = [sorted(set(r[0] for r in op["rd"] + op["wr"] if r[0] in BANKS)) for op in ops]
    rng = np.random.default_rng(seed)
    best = None
    for k in range(cfg["FB"] + 1):
        r = one_pass(ops, deps, succ, cs, prio, cfg, c, banks)
        if best is None or r[0] < best[0]:
            best, bprio = r, prio
        if k < cfg["FB"]:
            prio = one_pass(ops, succ, deps, cs, r[3], cfg, c, banks)[3]
    tags = {}
    for i, op in enumerate(ops):
        if op["eng"]:
            tags.setdefault(op["tag"], []).append(i)
    groups = list(tags.values())
    cur, cprio = best[0], bprio
    for k in range(cfg["ITER"]):
        prio = list(cprio)
        if k % 4 == 3:
            fin = one_pass(ops, deps, succ, cs, prio, cfg, c, banks)[3]
            amp = float(rng.random()) * cfg["STEP"] / 2
            prio = one_pass(ops, succ, deps, cs, [f + float(x) * amp for f, x in zip(fin, rng.random(n))], cfg, c, banks)[3]
        for t in rng.integers(0, len(groups), int(rng.integers(1, 4))):
            s = float(rng.normal()) * cfg["STEP"]
            one = int(rng.integers(0, 12))
            for i in (groups[t][one:one + 1] if one < len(groups[t]) else groups[t]):
                prio[i] += s
        r = one_pass(ops, deps, succ, cs, prio, cfg, c, banks)
        if r[0] <= cur + 600.0 * (1.0 - k / cfg["ITER"]) * float(rng.random()):
            cur, cprio = r[0], prio
        if r[0] < best[0]:
            best = r
    return polish(ops, deps, succ, cs, banks, best[1], cfg, c, rng)


def polish(ops, deps, succ, cs, banks, order, cfg, c, rng):
    n = len(ops)
    eng = [op["eng"] for op in ops]
    dl = [[(j, (0.0 if eng[i] == "P" else c["ls"]) if eng[i] == eng[j] and ops[j]["kind"] != "dma" else c["lx"])
           for j in deps[i]] for i in range(n)]
    where = {(op["visit"], op["tag"]): i for i, op in enumerate(ops)}
    lx = c["lx"]

    def run(order):
        free, users, fin, why = {}, {bk: {} for bk in BANKS}, [0.0] * n, [-1] * n
        for i in order:
            en = eng[i]
            t, w = free.get(en, (0.0, -1))
            for j, l in dl[i]:
                if fin[j] + l > t:
                    t, w = fin[j] + l, j
            for bk in banks[i]:
                u = users[bk]
                for e2, j in u.items():
                    if e2 != en and fin[j] + lx > t:
                        t, w = fin[j] + lx, j
                u[en] = i
            fin[i], why[i] = t + cs[i][1], w
            if en:
                free[en] = (t + cs[i][0], i)
        return max(fin) + cfg["SEC"] * sum(fin) / n, fin, why

    def move(order, u, v, ahead):
        a, b = order.index(u), order.index(v)
        if a >= b:
            return order
        mid = order[a:b + 1]
        if ahead:
            take = {v}
            for i in mid[::-1]:
                if i in take or not take.isdisjoint(succ[i]):
                    take.add(i)
            if u in take:
                return order
            return order[:a] + [i for i in mid if i in take] + [i for i in mid if i not in take] + order[b + 1:]
        take = {u}
        for i in mid:
            if i in take or not take.isdisjoint(deps[i]):
                take.add(i)
        if v in take:
            return order
        return order[:a] + [i for i in mid if i not in take] + [i for i in mid if i in take] + order[b + 1:]
    cur = run(order)
    best = (cur[0], order, max(cur[1]))
    for k in range(cfg["POLISH"]):
        i = cur[1].index(max(cur[1]))
        arcs = []
        while cur[2][i] >= 0:
            if cur[2][i] not in deps[i]:
                arcs.append((cur[2][i], i))
            i = cur[2][i]
        if not arcs:
            break
        s = int(rng.integers(0, len(arcs)))
        u, v = arcs[s]
        for _ in range(int(rng.integers(0, 4))):
            if s + 1 < len(arcs) and arcs[s + 1][1] == u:
                s += 1
                u = arcs[s][0]
        if rng.random() < cfg["FREE"]:
            s = int(rng.integers(1, n))
            v = order[s]
            mates = [i for i in order[max(0, s - 60):s] if eng[i] == eng[v]]
            if not eng[v] or not mates:
                continue
            u = mates[-1 - int(rng.integers(0, min(len(mates), 12)))]
            if rng.random() < cfg["FAR"]:
                u = order[max(0, s - int(rng.integers(1, 120)))]
        ahead, new = rng.random() < 0.5, order
        shifts = range(-NV, NV) if rng.random() < cfg["ALL"] and min(ops[u]["visit"], ops[v]["visit"]) >= 0 else [0]
        for d in shifts:
            u2, v2 = where.get((ops[u]["visit"] + d, ops[u]["tag"])), where.get((ops[v]["visit"] + d, ops[v]["tag"]))
            if u2 is not None and v2 is not None:
                new = move(new, u2, v2, ahead)
        r = run(new)
        if r[0] <= cur[0] - cfg["TEMP"] * (1.0 - k / cfg["POLISH"]) * float(np.log(rng.random() + 1e-12)):
            cur, order = r, new
            if r[0] < best[0]:
                best = (r[0], new, max(r[1]))
    users, alld = {bk: {} for bk in BANKS}, [None] * n
    for i in best[1]:
        alld[i] = set(deps[i])
        for bk in banks[i]:
            alld[i].update(j for e2, j in users[bk].items() if e2 != eng[i])
            users[bk][eng[i]] = i
    return best[2], best[1], alld


def one_pass(ops, deps, succ, cs, prio, cfg, c, banks):
    n = len(ops)
    left = [len(d) for d in deps]
    ready = [i for i in range(n) if not left[i]]
    free, fin, users, order, alld, base = {}, [0.0] * n, {}, [], [None] * n, [0.0] * n

    def lat(i, j):
        a, b = ops[i]["eng"], ops[j]["eng"]
        if a == b and ops[j]["kind"] != "dma":
            return 0.0 if a == "P" else c["ls"]
        return c["lx"]
    eng, lx, est = [op["eng"] for op in ops], c["lx"], [0.0] * n
    while ready:
        t0, i0 = 1e30, -1
        for i in ready:
            t, f = base[i], free.get(eng[i], 0.0)
            if f > t:
                t = f
            for bk in banks[i]:
                for en, j in users.get(bk, {}).items():
                    if en != eng[i] and fin[j] + lx > t:
                        t = fin[j] + lx
            est[i] = t
            if t < t0:
                t0, i0 = t, i
        i, e0, t0 = i0, eng[i0], t0 + cfg["SLACK"]
        for k in ready:
            if prio[k] > prio[i] and est[k] <= t0 and eng[k] == e0:
                i = k
        d = set(deps[i])
        for bk in banks[i]:
            d.update(j for en, j in users.get(bk, {}).items() if en != ops[i]["eng"])
            users.setdefault(bk, {})[ops[i]["eng"]] = i
        alld[i] = d
        fin[i] = est[i] + cs[i][1]
        if ops[i]["eng"]:
            free[ops[i]["eng"]] = est[i] + cs[i][0]
        order.append(i)
        ready.remove(i)
        for j in succ[i]:
            left[j] -= 1
            if not left[j]:
                base[j] = max(fin[k] + lat(j, k) for k in deps[j])
                ready.append(j)
    return max(fin), order, alld, fin


def periodic(ops, deps, cfg, c, off=None, per=None):
    n = len(ops)
    cs = costs(ops, c)
    succ = [set() for _ in range(n)]
    for i in range(n):
        for j in deps[i]:
            succ[j].add(i)
    eng = [op["eng"] for op in ops]
    dl = [[(j, (0.0 if eng[i] == "P" else c["ls"]) if eng[i] == eng[j] and ops[j]["kind"] != "dma" else c["lx"])
           for j in deps[i]] for i in range(n)]
    banks = [sorted(set(r[0] for r in op["rd"] + op["wr"] if r[0] in BANKS)) for op in ops]
    num = {}
    tag = [num.setdefault(op["tag"], len(num)) for op in ops]
    vis = [max(op["visit"], 0) for op in ops]
    heads = [[i for i in range(n) if ops[i]["visit"] == v and ops[i]["tag"][3] == "Hu"] for v in range(NV)]
    lx, dur, hold = c["lx"], [x[1] for x in cs], [x[0] for x in cs]
    if off is None:
        prio = [0.0] * n
        for i in range(n - 1, -1, -1):
            prio[i] = dur[i] + max([prio[j] + lx for j in succ[i]] + [0.0])
        best = None
        for k in range(cfg["FB"] + 1):
            r = one_pass(ops, deps, succ, cs, prio, cfg, c, banks)
            if best is None or r[0] < best[0]:
                best = r
            prio = one_pass(ops, succ, deps, cs, r[3], cfg, c, banks)[3]
        fin = best[3]
        hu = [min(fin[i] for i in h) for h in heads]
        per, off = (hu[-1] - hu[1]) / (NV - 2), [0.0] * len(num)
        for v in (-1, NV - 1, 2):
            for i in range(n):
                if ops[i]["visit"] == v:
                    off[tag[i]] = fin[i] - dur[i] - (hu[v] - hu[0] if v >= 0 else 0.0)

    def run(off):
        pr = [vis[i] * per + off[tag[i]] for i in range(n)]
        for i in range(n):
            for j in deps[i]:
                if pr[j] > pr[i]:
                    pr[i] = pr[j]
        order = sorted(range(n), key=lambda i: (pr[i], i))
        free, users, fin, why = {}, {bk: {} for bk in BANKS}, [0.0] * n, [-1] * n
        for i in order:
            en = eng[i]
            t, w = free.get(en, (0.0, -1))
            for j, l in dl[i]:
                if fin[j] + l > t:
                    t, w = fin[j] + l, j
            for bk in banks[i]:
                u = users[bk]
                for e2, j in u.items():
                    if e2 != en and fin[j] + lx > t:
                        t, w = fin[j] + lx, j
                u[en] = i
            fin[i], why[i] = t + dur[i], w
            if en:
                free[en] = (t + hold[i], i)
        return max(fin) + cfg["SEC"] * sum(fin) / n, fin, why, order, pr
    rng = np.random.default_rng(cfg["SEED"])
    cur = best = run(off)
    boff = off
    for k in range(cfg["ANNEAL"]):
        new, fin, why, pr, x = off[:], cur[1], cur[2], cur[4], rng.random()
        if x < 0.6:
            i, arcs = fin.index(max(fin)), []
            while why[i] >= 0:
                if why[i] not in deps[i]:
                    arcs.append((why[i], i))
                i = why[i]
            if not arcs:
                break
            u, v = arcs[int(rng.integers(0, len(arcs)))]
            if rng.random() < 0.5:
                lim, st = pr[u] - 1 - float(rng.random()) * 300, [v]
                while st:
                    a = st.pop()
                    if vis[a] * per + new[tag[a]] > lim or pr[a] > lim and a == v:
                        new[tag[a]] = min(new[tag[a]], lim - vis[a] * per)
                    st.extend(j for j in deps[a] if pr[j] > lim)
            else:
                new[tag[u]] = pr[v] + 1 + float(rng.random()) * 600 - vis[u] * per
        elif x < 0.95:
            for _ in range(int(rng.integers(1, 3))):
                new[int(rng.integers(0, len(off)))] += float(rng.normal()) * (500 if rng.random() < 0.6 else 2500)
        else:
            v = int(rng.integers(1, NV - 1))
            s0 = min(fin[i] - dur[i] - off[tag[i]] for i in heads[v])
            for i in range(n):
                if ops[i]["visit"] == v:
                    new[tag[i]] = fin[i] - dur[i] - s0
        r = run(new)
        if r[0] <= cur[0] - cfg["TEMP"] * (1.0 - k / cfg["ANNEAL"]) * float(np.log(rng.random() + 1e-12)):
            cur, off = r, new
            if r[0] < best[0]:
                best, boff = r, new
    users, alld = {bk: {} for bk in BANKS}, [None] * n
    for i in best[3]:
        alld[i] = set(deps[i])
        for bk in banks[i]:
            alld[i].update(j for e2, j in users[bk].items() if e2 != eng[i])
            users[bk][eng[i]] = i
    return max(best[1]), best[3], alld, boff, per


def names(ops):
    out, seen = [], {}
    for op in ops:
        nm, lo = (op["wr"] + op["rd"])[0][:2]
        lo = lo % L if nm in ("Tu", "ci", "co", "T2u") else lo % 16 * 16 if nm in ("bu", "bo") else 0 if nm == "bnd" else lo
        k = "%s.%s.%d" % (op["eng"] or "R", nm[0] if nm[0] in "Xd" and len(nm) == 2 else nm, lo)
        s = seen[op["visit"], k] = seen.get((op["visit"], k), 0) + 1
        out.append(k + ("#%d" % s if s > 1 else ""))
    return out


def arrange(ops, deps, c):
    n = len(ops)
    cs = costs(ops, c)
    eng = [op["eng"] for op in ops]
    banks = [sorted(set(r[0] for r in op["rd"] + op["wr"] if r[0] in BANKS)) for op in ops]
    pre = [[(j, (0.0 if eng[i] == "P" else c["ls"]) if eng[i] == eng[j] and ops[j]["kind"] != "dma" else c["lx"])
            for j in sorted(deps[i])] for i in range(n)]
    idx = {(op["visit"], k): i for i, (op, k) in enumerate(zip(ops, names(ops)))}
    for e, seq in ORDER.items():
        chain = [idx.get((v + w.count("+") - w.count("-"), e + "." + w.rstrip("+-")))
                 for v in range(-1, NV + 1) for w in seq.split() if v + w.count("+") - w.count("-") >= 0]
        chain = [i for i in chain if i is not None]
        for a, b in zip(chain[:-1], chain[1:]):
            if a not in deps[b]:
                pre[b].append((a, 0.0))
    suc = [[] for _ in range(n)]
    for i in range(n):
        for j, l in pre[i]:
            suc[j].append((i, l))
    left = [len(p) for p in pre]
    topo = [i for i in range(n) if not left[i]]
    for i in topo:
        for j, l in suc[i]:
            left[j] -= 1
            if not left[j]:
                topo.append(j)
    tail = [0.0] * n
    for i in topo[::-1]:
        tail[i] = cs[i][1] + max([tail[j] + l for j, l in suc[i]] + [0.0])
    best = None
    for slack in (50.0, 100.0, 200.0, 300.0, 400.0, 600.0):
        left = [len(p) for p in pre]
        ready = [i for i in range(n) if not left[i]]
        free, users, order, alld = {}, {bk: {} for bk in BANKS}, [], [None] * n
        fin, base, est = [0.0] * n, [0.0] * n, [0.0] * n
        while ready:
            for i in ready:
                est[i] = max([base[i], free.get(eng[i], 0.0)]
                             + [fin[j] + c["lx"] for bk in banks[i] for en, j in users[bk].items() if en != eng[i]])
            i0 = min(ready, key=lambda k: est[k])
            i = max((k for k in ready if eng[k] == eng[i0] and est[k] <= est[i0] + slack), key=lambda k: tail[k])
            alld[i] = set(deps[i])
            for bk in banks[i]:
                alld[i].update(j for en, j in users[bk].items() if en != eng[i])
                users[bk][eng[i]] = i
            fin[i] = est[i] + cs[i][1]
            if eng[i]:
                free[eng[i]] = est[i] + cs[i][0]
            order.append(i)
            ready.remove(i)
            for j, l in suc[i]:
                left[j] -= 1
                if not left[j]:
                    base[j] = max(fin[k] + l2 for k, l2 in pre[j])
                    ready.append(j)
        if best is None or max(fin) < best[0]:
            best = (max(fin), order, alld)
    return best


ORDER = {
    "V": "Hu.128 wI.0- bI.0- c1.192 c1.128 tk.192 u.192 Hu.0 tk.128 T1u.192 u.128 c1.64 T1u.128 c1.0 tk.64 u.64 mn.128 T1u.64 "
         "tk.0 a1.128 u.0 qI.128 nI.128 T1u.0 nu.128 mx.128 E.0 E.1 mn.0 mx.0 a0.128 rel.128 qI.0 nI.0 sg0.128 sg1.128 sg2.128 "
         "sg3.128 nu.0 uI.0 o1.0 uA.0 nr.128 jI.0 a1.256 T2.128 tt.0 tt.0#2 kT.128 ks.128 tt.0#3 kI.128 rel.0 kA.128 tt.0#4 "
         "klo.128 w.128 sg1.0 sg0.0 sg2.0 wI.128 s8i.0 bI.128 sg3.0 X.0 nr.0 a0.256 T2.0 tt.0#5 tt.0#6 tt.0#7 kT.0 ks.0 kI.0 "
         "kA.0 klo.0 w.0 tt.0#8",
    "S": "x.192 r1.0- x.128 brC.128 r2.0- bnd.0- x.64 x.0 z.192 z.128 sC.0 brC.0 FB.0 z.64 z.0 e.192 e.128 hh.128 ab0.128 "
         "ab1.128 ab2.128 ab3.128 e.0 e.64 s8.0 ab0.0 hh.0 ab1.0 ab2.0 ab3.0",
}


def close_groups(ops, order):
    final = {ops[i]["group"]: i for i in order if "group" in ops[i]}
    for i, op in enumerate(ops):
        if "group" in op:
            op["stop"][0] = final[op["group"]] == i


PLAN = {}


def rank_program(g, core, T, topo):
    rank = T.rank_of(core)
    if rank is None:
        return
    nxt = T.cores[(rank + 1) % len(T.cores)]
    ops = build(g, T, topo.addr(nxt)[:2], topo.engines(core, nxt), CFG)
    if not PLAN:
        deps = data_deps(ops)
        PLAN["p"] = arrange(ops, deps, COST)
        PLAN["raw"] = [op["raw"] for op in ops]
    order, deps = PLAN["p"][1:3]
    raw = PLAN["raw"]
    close_groups(ops, order)
    q = {"V": g.vector, "S": g.scalar, "P": g.tensor, "G": g, "Y": g.sync}
    known = {k: {} for k in q}
    count = {k: 0 for k in "VSPG"}
    token, clock, sent, ends = {}, {}, 0, {}
    for i in order:
        op = ops[i]
        en = op["eng"]
        if en is None:
            token[i], clock[i] = (op["sem"], op["cnt"]), {op["sem"]: op["cnt"]}
            ends[op["sem"]] = op["cnt"]
            continue
        need = {}
        for j in deps[i]:
            if en == "P" and ops[j]["eng"] == "P":
                continue
            if CFG["WAW"] and en in "VS" and ops[j]["eng"] == en and ops[j]["kind"] != "dma" and j not in raw[i]:
                continue
            if j in token and token[j][1] > need.get(token[j][0], (0, 0))[0]:
                need[token[j][0]] = (token[j][1], j)
        kn = known[en]
        for s, (val, j) in sorted(need.items(), key=lambda t: -len(clock[t[1][1]])):
            if kn.get(s, 0) < val:
                q[en].wait_ge(T.sem[s], val)
                for s2, v2 in clock[j].items():
                    kn[s2] = max(kn.get(s2, 0), v2)
        r = op["fn"]()
        if op["kind"] == "send":
            sent += op["cnt"]
            continue
        if op["kind"] == "dma":
            r.then_inc(T.sem[op["sem"]], 16)
            token[i] = (op["sem"], 16)
        else:
            r.then_inc(T.sem[en], 1)
            count[en] += 1
            token[i] = (en, count[en])
        ends[token[i][0]] = token[i][1]
        clock[i] = dict(kn)
        clock[i][token[i][0]] = token[i][1]
    ends["sent"] = sent
    for s, val in ends.items():
        if known["G"].get(s, 0) < val:
            g.wait_ge(T.sem[s], val)
